import numpy as np
import ml_dtypes


def mxq(x, axis, fmt="e4m3"):
    dtype, down = {"e4m3": (ml_dtypes.float8_e4m3fn, 7), "e5m2": (ml_dtypes.float8_e5m2, 14)}[fmt]
    v = np.moveaxis(np.asarray(x, np.float32).astype(ml_dtypes.bfloat16).astype(np.float64), axis, -1)
    blocks = v.reshape(v.shape[:-1] + (-1, 32))
    amax = np.abs(blocks).max(-1, keepdims=True)
    byte = np.maximum(np.where(amax > 0, np.frexp(amax)[1] - 1 + 127, 0) - down, 1)
    scale = np.exp2(byte - 127.0)
    codes = (blocks / scale).astype(np.float32).astype(dtype).astype(np.float64)
    return np.moveaxis((codes * scale).reshape(v.shape), -1, axis)


WIDE = False


def mx_kscale(k):
    if not WIDE:
        return np.ones(k)
    levels = np.array([10, -10, 5, -5, 0])
    if k % 512:
        return np.exp2(np.random.permutation(np.resize(levels, k // 32))).repeat(32)
    a = np.empty((k // 512, 16))
    for p in range(k // 512):
        a[p, :8] = np.random.permutation(np.resize(levels, 8))
        for g in range(8):
            far = levels[np.abs(levels - a[p, g]) >= 10]
            a[p, g + 8] = far[np.random.randint(len(far))]
    return np.exp2(a.ravel()).repeat(32)


def f64(x):
    return np.asarray(x).astype(np.float64)


def striped(idx):
    return np.tile(idx.reshape(-1, 16).T, (8, 1)).astype(np.uint16)


def unstriped(offs):
    return offs[:16].T.reshape(-1).astype(np.int64)


def pack_weight(w):
    k, n = w.shape
    w = f64(np.asarray(w, np.float32).astype(ml_dtypes.bfloat16)).reshape(k // 32, 32, n)
    amax = np.abs(w).max(1)
    byte = np.clip(np.where(amax > 0, np.frexp(amax)[1] - 1 + 127 - 7, 1), 1, 254)
    scaled = (w * np.exp2(127.0 - byte)[:, None, :]).reshape(k, n).astype(np.float32)
    words = np.ascontiguousarray(scaled.reshape(k // 512, 128, 4, n).transpose(0, 1, 3, 2)).astype(ml_dtypes.float8_e4m3fn).view(np.uint8)
    return words, np.ascontiguousarray(byte.astype(np.uint8).reshape(k // 512, 16, n))


def unpack_weight(words, scales):
    g, p, n, _ = words.shape
    vals = np.ascontiguousarray(words).view(ml_dtypes.float8_e4m3fn).astype(np.float64) * np.repeat(np.exp2(scales.astype(np.float64) - 127.0), 8, axis=1)[..., None]
    return vals.transpose(0, 1, 3, 2).reshape(g * 512, n)


K, T, S, H, N, V = 1024, 1024, 512, 512, 128, 256
P = 2 ** 7


def setup_inputs():
    n = np.random.standard_normal
    s = mx_kscale(K)[:, None]
    u = mx_kscale(H)
    perm = np.random.permutation(S)
    packed_xT = pack_weight(n((K, T)) * s)
    packed_w2 = pack_weight(n((H, N)) / np.sqrt(H) / u[:, None])
    return {
        "x_words": packed_xT[0],
        "x_scales": packed_xT[1],
        "w1": (n((K, H)) / np.sqrt(K) / s * u).astype(np.float32),
        "w2_words": packed_w2[0],
        "w2_scales": packed_w2[1],
        "gate": (np.tile(np.random.uniform(0.2, 1.0, V), (P, 1))).astype(np.float32),
        "back": (np.tile(np.random.uniform(0.5, 1.5, V), (P, 1))).astype(np.float32),
        "offs": striped(np.random.permutation(T)[:S]),
        "ka": striped(perm[:V]),
        "kb": striped(perm[V:]),
    }


def reference(x_words, x_scales, w1, w2_words, w2_scales, gate, back, offs, ka, kb):
    xq = unpack_weight(x_words, x_scales)[:, unstriped(offs)]
    h = mxq(f64(w1), 0, "e4m3").T @ xq
    z = h[:, unstriped(ka)] + h[:, unstriped(kb)] * f64(gate)[:1]
    y = unpack_weight(w2_words, w2_scales).T @ mxq(z, 0, "e4m3")
    yb = y * f64(back)[:1]
    out = np.zeros((N, S))
    out[:, unstriped(ka)] = y
    res = out.copy()
    res[:, unstriped(kb)] = yb
    return res

@@ -1,0 +1,196 @@
+from contextlib import ExitStack
+
+import concourse.mybir as mybir
+
+K, T, S, H, N, V = 1024, 1024, 512, 512, 128, 256
+FLOPS = 2 * K * H * S + 2 * H * N * V
+
+F32 = mybir.dt.float32
+BF16 = mybir.dt.bfloat16
+I32 = mybir.dt.int32
+U32 = mybir.dt.uint32
+U16 = mybir.dt.uint16
+U8 = mybir.dt.uint8
+FP8X4 = mybir.dt.float8_e4m3fn_x4
+MULT = mybir.AluOpType.mult
+ADD = mybir.AluOpType.add
+
+P = 128
+PACK = 4
+PASSES = K // (P * PACK)
+HALF = V // 2
+
+
+def tile_picked_zunm_none_p_kernel(
+    tc, x_words, x_scales, w1, w2_words, w2_scales, gate, back, offs, ka, kb, out
+):
+    nc = tc.nc
+    with ExitStack() as ctx:
+        keep = ctx.enter_context(tc.tile_pool(name="keep", bufs=1))
+        psum = ctx.enter_context(tc.psum_pool(name="psum", bufs=1))
+
+        offs_sb = keep.tile([P, S // 16], U16, name="offs_sb")
+        ka_sb = keep.tile([P, V // 16], U16, name="ka_sb")
+        kb_sb = keep.tile([P, V // 16], U16, name="kb_sb")
+        xs_all = keep.tile([P, T], U8, name="xs_all", align_bytes=64)
+        w2s = keep.tile([P, N], U8, name="w2s", align_bytes=64)
+        w2c = keep.tile([P, N], I32, name="w2c", align_bytes=64)
+        xw_all = [keep.tile([P, T], I32, name="xw_all%d" % g, align_bytes=64) for g in range(PASSES)]
+        chunks = [(0, 0, 0, P), (0, 1, 0, P), (1, 0, 0, P), (1, 1, 0, 64), (1, 1, 64, P)]
+        w_raw = [
+            keep.tile([P, 2, PACK * (hi - lo)], F32, name="w_raw%d" % i) for i, (g, u, lo, hi) in enumerate(chunks)
+        ]
+        gate_sb = [keep.tile([P, HALF], F32, name="gate%d" % c) for c in range(2)]
+        back_sb = keep.tile([P, V], F32, name="back_sb")
+
+        nc.gpsimd.memset(xs_all[:].bitcast(I32), 0)
+        nc.gpsimd.memset(w2s[:].bitcast(I32), 0)
+
+        def load_words(g):
+            nc.sync.dma_start(xw_all[g][:], x_words[g].rearrange("p n t -> p (n t)").bitcast(I32))
+
+        nc.sync.dma_start(offs_sb[:], offs)
+        for i, (g, u, lo, hi) in enumerate(chunks):
+            rows = w1[512 * g : 512 * (g + 1), :].rearrange("(p j) c -> p j c", j=PACK)
+            nc.sync.dma_start(w_raw[i][:], rows[:, 2 * u : 2 * u + 2, PACK * lo : PACK * hi])
+            if i == 0:
+                for q in range(4):
+                    nc.sync.dma_start(
+                        xs_all[32 * q : 32 * q + 8, :].bitcast(I32),
+                        x_scales[:, 4 * q : 4 * q + 4, :].bitcast(I32),
+                    )
+                load_words(0)
+        load_words(1)
+        nc.sync.dma_start(kb_sb[:], kb)
+        nc.sync.dma_start(gate_sb[0][:], gate[:, 0:HALF])
+        nc.sync.dma_start(ka_sb[:], ka)
+        nc.sync.dma_start(gate_sb[1][:], gate[:, HALF:V])
+        nc.sync.dma_start(w2c[:], w2_words[0].rearrange("p n t -> p (n t)").bitcast(I32))
+        for q in range(4):
+            nc.sync.dma_start(
+                w2s[32 * q : 32 * q + 4, :].bitcast(I32),
+                w2_scales[0, 4 * q : 4 * q + 4, :].bitcast(I32),
+            )
+        nc.sync.dma_start(back_sb[:], back)
+
+        xw = [keep.tile([P, S], U32, name="xw%d" % g, align_bytes=64) for g in range(PASSES)]
+        xs = keep.tile([P, S], U8, name="xs", align_bytes=64)
+        w_bf = [
+            [keep.tile([P, 2 * H], BF16, name="w_bf%d%d" % (g, r), align_bytes=64) for r in range(2)]
+            for g in range(PASSES)
+        ]
+        wc = [keep.tile([P, H], U32, name="wc%d" % g, align_bytes=64) for g in range(PASSES)]
+        ws = [keep.tile([P, H], U8, name="ws%d" % g, align_bytes=64) for g in range(PASSES)]
+
+        def gather_words(g, lo, hi):
+            nc.vector.tensor_copy(
+                xw[g][:, lo:hi], xw_all[g][:].bitcast(U32).indirect(offs_sb[:, lo // 16 : hi // 16])
+            )
+
+        def cast(engine_copy, i, r):
+            g, u, lo, hi = chunks[i]
+            dst = w_bf[g][r][:].rearrange("p (t m j) -> p m t j", t=2, j=PACK)
+            src = w_raw[i][:].rearrange("p j (m t) -> p m t j", t=PACK)
+            engine_copy(dst[:, lo:hi, :, 2 * u : 2 * u + 2], src[:, :, 2 * r : 2 * r + 2, :])
+
+        def quantize_w(g, r):
+            nc.vector.quantize_mx(
+                out=wc[g][:, 2 * P * r : 2 * P * (r + 1)].bitcast(FP8X4),
+                scales=ws[g][:, 2 * P * r : 2 * P * (r + 1)],
+                in_=w_bf[g][r][:],
+            )
+
+        def product(acc, g, t, lo, hi):
+            nc.tensor.matmul_mx(
+                out=acc,
+                lhsT=wc[g][:, P * t : P * (t + 1)].bitcast(FP8X4),
+                lhsT_scale=ws[g][:, P * t : P * (t + 1)],
+                rhs=xw[g][:, lo:hi].bitcast(FP8X4),
+                rhs_scale=xs[4 * g : P, lo:hi],
+                start=(g == 0),
+                stop=(g == PASSES - 1),
+            )
+
+        pieces = [(0, 0, 256), (0, 256, 512), (1, 0, 256), (1, 256, 512), (2, 0, 512), (3, 0, 512)]
+        accs = [psum.tile([P, hi - lo], F32, name="acc%d" % i) for i, (t, lo, hi) in enumerate(pieces)]
+        h = [keep.tile([P, S], F32, name="h%d" % t) for t in range(PACK)]
+
+        nc.vector.tensor_copy(xs[:], xs_all[:].indirect(offs_sb[:]))
+        gather_words(0, 0, S)
+        cast(nc.scalar.copy, 0, 0)
+        cast(nc.scalar.copy, 0, 1)
+        cast(nc.vector.tensor_copy, 1, 0)
+        cast(nc.scalar.copy, 1, 1)
+        quantize_w(0, 0)
+        quantize_w(0, 1)
+        for acc, (t, lo, hi) in zip(accs, pieces):
+            product(acc[:], 0, t, lo, hi)
+        for i in (2, 3, 4):
+            cast(nc.vector.tensor_copy, i, 0)
+            cast(nc.scalar.copy, i, 1)
+        quantize_w(1, 0)
+        gather_words(1, 0, 256)
+        gather_words(1, 256, 512)
+        quantize_w(1, 1)
+        for acc, (t, lo, hi) in zip(accs, pieces):
+            product(acc[:], 1, t, lo, hi)
+            nc.scalar.copy(h[t][:, lo:hi], acc[:])
+
+        window = keep.tile([P, S], F32, name="window")
+        cols = HALF // 16
+
+        def entries(list_sb, c):
+            return list_sb[:, c * cols : (c + 1) * cols]
+
+        gated = {}
+
+        def gather_gated(c, t, tag):
+            gated[c, t] = keep.tile([P, HALF], F32, name="gated%d%d" % (c, t), tag=tag)
+            nc.vector.tensor_tensor(gated[c, t][:], h[t][:].indirect(entries(kb_sb, c)), gate_sb[c][:], MULT)
+
+        def gather_add(z, c, t):
+            nc.vector.tensor_tensor(z[:, t, :], h[t][:].indirect(entries(ka_sb, c)), gated[c, t][:], ADD)
+
+        def second_product(z, c):
+            z_bf = keep.tile([P, HALF, PACK], BF16, name="z_bf%d" % c, align_bytes=64)
+            nc.scalar.copy(z_bf[:], z[:].rearrange("p t v -> p v t"))
+            zc = keep.tile([P, HALF], U32, name="zc%d" % c, align_bytes=64)
+            zs = keep.tile([P, HALF], U8, name="zs%d" % c, align_bytes=64)
+            nc.vector.quantize_mx(out=zc[:].bitcast(FP8X4), scales=zs[:], in_=z_bf[:].rearrange("p v t -> p (v t)"))
+            y_acc = psum.tile([P, HALF], F32, name="y_acc%d" % c)
+            nc.tensor.matmul_mx(
+                out=y_acc[:],
+                lhsT=w2c[:].bitcast(FP8X4),
+                lhsT_scale=w2s[:],
+                rhs=zc[:].bitcast(FP8X4),
+                rhs_scale=zs[:],
+                start=True,
+                stop=True,
+            )
+            return y_acc
+
+        for t in range(PACK):
+            gather_gated(0, t, "slot%d" % t)
+            if t in (0, 3):
+                gather_gated(1, t, "own%d" % t)
+        z0 = keep.tile([P, PACK, HALF], F32, name="z0", tag="gate0")
+        for t in range(PACK):
+            gather_add(z0, 0, t)
+        y_acc0 = second_product(z0, 0)
+        y0 = keep.tile([P, HALF], F32, name="y0")
+        nc.scalar.copy(y0[:], y_acc0[:])
+        gather_gated(1, 1, "slot0")
+        gather_gated(1, 2, "slot1")
+        z1 = keep.tile([P, PACK, HALF], F32, name="z1", tag="slot3")
+        for t in (0, 3, 1, 2):
+            gather_add(z1, 1, t)
+        y_acc1 = second_product(z1, 1)
+        y0_again = keep.tile([P, HALF], F32, name="y0_again", tag="slot3")
+        nc.scalar.copy(y0_again[:], y_acc0[:])
+        y1 = keep.tile([P, HALF], F32, name="y1")
+        nc.scalar.copy(y1[:], y_acc1[:])
+        nc.vector.tensor_copy(window[:].indirect(entries(ka_sb, 0)), y0[:])
+        nc.vector.tensor_tensor(window[:].indirect(entries(kb_sb, 0)), y0_again[:], back_sb[:, 0:HALF], MULT)
+        nc.vector.tensor_copy(window[:].indirect(entries(ka_sb, 1)), y1[:])
+        nc.vector.tensor_tensor(window[:].indirect(entries(kb_sb, 1)), y1[:], back_sb[:, HALF:V], MULT)
+        nc.sync.dma_start(out, window[:])

@@ -1,6 +1,7 @@
 from contextlib import ExitStack
 
 import concourse.mybir as mybir
+from concourse.masks import make_identity
 
 K, T, S, H, N, V = 1024, 1024, 512, 512, 128, 256
 FLOPS = 2 * K * H * S + 2 * H * N * V
@@ -19,6 +20,7 @@ P = 128
 PACK = 4
 PASSES = K // (P * PACK)
 HALF = V // 2
+TILES = H // P
 
 
 def tile_picked_zunm_none_p_kernel(
@@ -36,34 +38,37 @@ def tile_picked_zunm_none_p_kernel(
         w2s = keep.tile([P, N], U8, name="w2s", align_bytes=64)
         w2c = keep.tile([P, N], I32, name="w2c", align_bytes=64)
         xw_all = [keep.tile([P, T], I32, name="xw_all%d" % g, align_bytes=64) for g in range(PASSES)]
-        chunks = [(0, 0, 0, P), (0, 1, 0, P), (1, 0, 0, P), (1, 1, 0, 64), (1, 1, 64, P)]
-        w_raw = [
-            keep.tile([P, 2, PACK * (hi - lo)], F32, name="w_raw%d" % i) for i, (g, u, lo, hi) in enumerate(chunks)
-        ]
+        w_raw = [[keep.tile([P, PACK, 2 * P], F32, name="w_raw%d%d" % (w, g), align_bytes=64) for g in range(PASSES)] for w in range(2)]
+        ident = keep.tile([P, P], F32, name="ident")
         gate_sb = [keep.tile([P, HALF], F32, name="gate%d" % c) for c in range(2)]
         back_sb = keep.tile([P, V], F32, name="back_sb")
 
         nc.gpsimd.memset(xs_all[:].bitcast(I32), 0)
         nc.gpsimd.memset(w2s[:].bitcast(I32), 0)
+        make_identity(nc, ident[:])
 
         def load_words(g):
             nc.sync.dma_start(xw_all[g][:], x_words[g].rearrange("p n t -> p (n t)").bitcast(I32))
 
-        nc.sync.dma_start(offs_sb[:], offs)
-        for i, (g, u, lo, hi) in enumerate(chunks):
+        def load_w(w, g):
             rows = w1[512 * g : 512 * (g + 1), :].rearrange("(p j) c -> p j c", j=PACK)
-            nc.sync.dma_start(w_raw[i][:], rows[:, 2 * u : 2 * u + 2, PACK * lo : PACK * hi])
-            if i == 0:
-                for q in range(4):
-                    nc.sync.dma_start(
-                        xs_all[32 * q : 32 * q + 8, :].bitcast(I32),
-                        x_scales[:, 4 * q : 4 * q + 4, :].bitcast(I32),
-                    )
-                load_words(0)
+            nc.sync.dma_start(w_raw[w][g][:], rows[:, :, 2 * P * w : 2 * P * (w + 1)])
+
+        nc.sync.dma_start(offs_sb[:], offs)
+        load_w(0, 0)
+        for q in range(4):
+            nc.sync.dma_start(
+                xs_all[32 * q : 32 * q + 8, :].bitcast(I32),
+                x_scales[:, 4 * q : 4 * q + 4, :].bitcast(I32),
+            )
+        load_words(0)
+        load_w(0, 1)
         load_words(1)
         nc.sync.dma_start(kb_sb[:], kb)
-        nc.sync.dma_start(gate_sb[0][:], gate[:, 0:HALF])
         nc.sync.dma_start(ka_sb[:], ka)
+        nc.sync.dma_start(gate_sb[0][:], gate[:, 0:HALF])
+        load_w(1, 0)
+        load_w(1, 1)
         nc.sync.dma_start(gate_sb[1][:], gate[:, HALF:V])
         nc.sync.dma_start(w2c[:], w2_words[0].rearrange("p n t -> p (n t)").bitcast(I32))
         for q in range(4):
@@ -73,68 +78,48 @@ def tile_picked_zunm_none_p_kernel(
             )
         nc.sync.dma_start(back_sb[:], back)
 
-        xw = [keep.tile([P, S], U32, name="xw%d" % g, align_bytes=64) for g in range(PASSES)]
+        xw = {}
         xs = keep.tile([P, S], U8, name="xs", align_bytes=64)
-        w_bf = [
-            [keep.tile([P, 2 * H], BF16, name="w_bf%d%d" % (g, r), align_bytes=64) for r in range(2)]
-            for g in range(PASSES)
-        ]
-        wc = [keep.tile([P, H], U32, name="wc%d" % g, align_bytes=64) for g in range(PASSES)]
-        ws = [keep.tile([P, H], U8, name="ws%d" % g, align_bytes=64) for g in range(PASSES)]
+        wc, ws = {}, {}
 
-        def gather_words(g, lo, hi):
-            nc.vector.tensor_copy(
-                xw[g][:, lo:hi], xw_all[g][:].bitcast(U32).indirect(offs_sb[:, lo // 16 : hi // 16])
+        def gather_words(g, tag):
+            xw[g] = keep.tile([P, S], U32, name="xw%d" % g, tag=tag, align_bytes=64)
+            nc.vector.tensor_copy(xw[g][:], xw_all[g][:].bitcast(U32).indirect(offs_sb[:]))
+
+        def cast_w(w, g, s_lo, s_hi, engine_copy, tag):
+            w_bf = keep.tile([P, (s_hi - s_lo) * H], BF16, name="w_bf%d%d%d" % (w, g, s_lo), tag=tag, align_bytes=64)
+            engine_copy(
+                w_bf[:].rearrange("p (s q e j) -> p q s j e", q=64, e=2, j=PACK),
+                w_raw[w][g][:].rearrange("p j (q s e) -> p q s j e", s=2, e=2)[:, :, s_lo:s_hi],
             )
+            return w_bf
 
-        def cast(engine_copy, i, r):
-            g, u, lo, hi = chunks[i]
-            dst = w_bf[g][r][:].rearrange("p (t m j) -> p m t j", t=2, j=PACK)
-            src = w_raw[i][:].rearrange("p j (m t) -> p m t j", t=PACK)
-            engine_copy(dst[:, lo:hi, :, 2 * u : 2 * u + 2], src[:, :, 2 * r : 2 * r + 2, :])
+        def quantize_w(w, g, s_lo, s_hi, w_bf):
+            width = P * (s_hi - s_lo)
+            codes = keep.tile([P, width], U32, name="wc%d%d%d" % (w, g, s_lo), align_bytes=64)
+            scales = keep.tile([P, width], U8, name="ws%d%d%d" % (w, g, s_lo), align_bytes=64)
+            nc.vector.quantize_mx(out=codes[:].bitcast(FP8X4), scales=scales[:], in_=w_bf[:])
+            for s in range(s_lo, s_hi):
+                wc[w, g, s] = codes[:, P * (s - s_lo) : P * (s - s_lo + 1)]
+                ws[w, g, s] = scales[:, P * (s - s_lo) : P * (s - s_lo + 1)]
 
-        def quantize_w(g, r):
-            nc.vector.quantize_mx(
-                out=wc[g][:, 2 * P * r : 2 * P * (r + 1)].bitcast(FP8X4),
-                scales=ws[g][:, 2 * P * r : 2 * P * (r + 1)],
-                in_=w_bf[g][r][:],
-            )
+        h = []
 
-        def product(acc, g, t, lo, hi):
-            nc.tensor.matmul_mx(
-                out=acc,
-                lhsT=wc[g][:, P * t : P * (t + 1)].bitcast(FP8X4),
-                lhsT_scale=ws[g][:, P * t : P * (t + 1)],
-                rhs=xw[g][:, lo:hi].bitcast(FP8X4),
-                rhs_scale=xs[4 * g : P, lo:hi],
-                start=(g == 0),
-                stop=(g == PASSES - 1),
-            )
-
-        pieces = [(0, 0, 256), (0, 256, 512), (1, 0, 256), (1, 256, 512), (2, 0, 512), (3, 0, 512)]
-        accs = [psum.tile([P, hi - lo], F32, name="acc%d" % i) for i, (t, lo, hi) in enumerate(pieces)]
-        h = [keep.tile([P, S], F32, name="h%d" % t) for t in range(PACK)]
-
-        nc.vector.tensor_copy(xs[:], xs_all[:].indirect(offs_sb[:]))
-        gather_words(0, 0, S)
-        cast(nc.scalar.copy, 0, 0)
-        cast(nc.scalar.copy, 0, 1)
-        cast(nc.vector.tensor_copy, 1, 0)
-        cast(nc.scalar.copy, 1, 1)
-        quantize_w(0, 0)
-        quantize_w(0, 1)
-        for acc, (t, lo, hi) in zip(accs, pieces):
-            product(acc[:], 0, t, lo, hi)
-        for i in (2, 3, 4):
-            cast(nc.vector.tensor_copy, i, 0)
-            cast(nc.scalar.copy, i, 1)
-        quantize_w(1, 0)
-        gather_words(1, 0, 256)
-        gather_words(1, 256, 512)
-        quantize_w(1, 1)
-        for acc, (t, lo, hi) in zip(accs, pieces):
-            product(acc[:], 1, t, lo, hi)
-            nc.scalar.copy(h[t][:, lo:hi], acc[:])
+        def product(w, s, tag):
+            u = 2 * w + s
+            acc = psum.tile([P, S], F32, name="acc%d" % u, tag="bank%d" % u)
+            for g in range(PASSES):
+                nc.tensor.matmul_mx(
+                    out=acc[:],
+                    lhsT=wc[w, g, s].bitcast(FP8X4),
+                    lhsT_scale=ws[w, g, s],
+                    rhs=xw[g][:].bitcast(FP8X4),
+                    rhs_scale=xs[4 * g : P, :],
+                    start=(g == 0),
+                    stop=(g == PASSES - 1),
+                )
+            h.append(keep.tile([P, S], F32, name="h%d" % u, tag=tag, align_bytes=64))
+            nc.scalar.copy(h[u][:], acc[:])
 
         window = keep.tile([P, S], F32, name="window")
         cols = HALF // 16
@@ -142,22 +127,32 @@ def tile_picked_zunm_none_p_kernel(
         def entries(list_sb, c):
             return list_sb[:, c * cols : (c + 1) * cols]
 
-        gated = {}
+        def look_up(c, u, pair):
+            nc.vector.tensor_tensor(pair[:, 0, :], h[u][:].indirect(entries(kb_sb, c)), gate_sb[c][:], MULT)
+            nc.vector.tensor_copy(pair[:, 1, :], h[u][:].indirect(entries(ka_sb, c)))
 
-        def gather_gated(c, t, tag):
-            gated[c, t] = keep.tile([P, HALF], F32, name="gated%d%d" % (c, t), tag=tag)
-            nc.vector.tensor_tensor(gated[c, t][:], h[t][:].indirect(entries(kb_sb, c)), gate_sb[c][:], MULT)
+        def turn_and_add(zt, pair):
+            for i in range(2):
+                nc.tensor.matmul(zt, pair[:, i, :], ident[:], is_transpose=True, start=(i == 0), stop=(i == 1))
 
-        def gather_add(z, c, t):
-            nc.vector.tensor_tensor(z[:, t, :], h[t][:].indirect(entries(ka_sb, c)), gated[c, t][:], ADD)
-
-        def second_product(z, c):
-            z_bf = keep.tile([P, HALF, PACK], BF16, name="z_bf%d" % c, align_bytes=64)
-            nc.scalar.copy(z_bf[:], z[:].rearrange("p t v -> p v t"))
+        def second_product(c, pairs, bank):
+            zt_bf = keep.tile([P, H], BF16, name="zt_bf%d" % c)
+            for lo, hi, zt_bank in ((0, 3, "bank%d" % (4 + c)), (3, 4, "bank%d" % (5 - c))):
+                zt = psum.tile([P, P * (hi - lo)], F32, name="zt%d_%d" % (c, lo), tag=zt_bank)
+                for u in range(lo, hi):
+                    block = 2 * (u % 2) + u // 2 - lo
+                    turn_and_add(zt[:, P * block : P * (block + 1)], pairs[:, u])
+                nc.scalar.copy(zt_bf[:, P * lo : P * hi], zt[:])
+            words = zt_bf[:].bitcast(F32)
+            turned = psum.tile([P, 2, HALF], F32, name="turned%d" % c, tag="bank6")
+            for r in range(2):
+                nc.tensor.transpose(turned[:, r, :], words[:, P * r : P * (r + 1)], ident[:])
+            z_bf = keep.tile([P, HALF * PACK], BF16, name="z_bf%d" % c, align_bytes=64)
+            nc.scalar.copy(z_bf[:].bitcast(F32).rearrange("p (v r) -> p v r", r=2), turned[:].rearrange("p r v -> p v r"))
             zc = keep.tile([P, HALF], U32, name="zc%d" % c, align_bytes=64)
             zs = keep.tile([P, HALF], U8, name="zs%d" % c, align_bytes=64)
-            nc.vector.quantize_mx(out=zc[:].bitcast(FP8X4), scales=zs[:], in_=z_bf[:].rearrange("p v t -> p (v t)"))
-            y_acc = psum.tile([P, HALF], F32, name="y_acc%d" % c)
+            nc.vector.quantize_mx(out=zc[:].bitcast(FP8X4), scales=zs[:], in_=z_bf[:])
+            y_acc = psum.tile([P, HALF], F32, name="y_acc%d" % c, tag=bank)
             nc.tensor.matmul_mx(
                 out=y_acc[:],
                 lhsT=w2c[:].bitcast(FP8X4),
@@ -169,23 +164,36 @@ def tile_picked_zunm_none_p_kernel(
             )
             return y_acc
 
-        for t in range(PACK):
-            gather_gated(0, t, "slot%d" % t)
-            if t in (0, 3):
-                gather_gated(1, t, "own%d" % t)
-        z0 = keep.tile([P, PACK, HALF], F32, name="z0", tag="gate0")
-        for t in range(PACK):
-            gather_add(z0, 0, t)
-        y_acc0 = second_product(z0, 0)
+
+        nc.vector.tensor_copy(xs[:], xs_all[:].indirect(offs_sb[:]))
+        gather_words(0, "xw0")
+        quantize_w(0, 0, 0, 2, cast_w(0, 0, 0, 2, nc.scalar.copy, "w_bf000"))
+        quantize_w(0, 1, 0, 1, cast_w(0, 1, 0, 1, nc.scalar.copy, "w_bf010"))
+        gather_words(1, "w_bf010")
+        quantize_w(0, 1, 1, 2, cast_w(0, 1, 1, 2, nc.scalar.copy, "w_bf011"))
+        by_scalar = cast_w(1, 0, 1, 2, nc.scalar.copy, "w_bf101")
+        by_vector = cast_w(1, 0, 0, 1, nc.vector.tensor_copy, "w_raw01")
+        quantize_w(1, 0, 0, 1, by_vector)
+        quantize_w(1, 0, 1, 2, by_scalar)
+        product(0, 0, "w_raw10")
+        by_scalar = cast_w(1, 1, 1, 2, nc.scalar.copy, "wc010")
+        by_vector = cast_w(1, 1, 0, 1, nc.vector.tensor_copy, "w_raw01")
+        quantize_w(1, 1, 0, 1, by_vector)
+        quantize_w(1, 1, 1, 2, by_scalar)
+        product(0, 1, "w_raw11")
+        product(1, 0, "h2")
+        product(1, 1, "h3")
+        first = keep.tile([P, TILES, 2, HALF], F32, name="first", tag="w_raw01", align_bytes=64)
+        for u in range(TILES):
+            look_up(0, u, first[:, u])
+        second = keep.tile([P, TILES, 2, HALF], F32, name="second", tag="gate0")
+        for u in range(TILES):
+            look_up(1, u, second[:, u])
+        y_acc0 = second_product(0, first, "bank7")
         y0 = keep.tile([P, HALF], F32, name="y0")
         nc.scalar.copy(y0[:], y_acc0[:])
-        gather_gated(1, 1, "slot0")
-        gather_gated(1, 2, "slot1")
-        z1 = keep.tile([P, PACK, HALF], F32, name="z1", tag="slot3")
-        for t in (0, 3, 1, 2):
-            gather_add(z1, 1, t)
-        y_acc1 = second_product(z1, 1)
-        y0_again = keep.tile([P, HALF], F32, name="y0_again", tag="slot3")
+        y_acc1 = second_product(1, second, "bank1")
+        y0_again = keep.tile([P, HALF], F32, name="y0_again", tag="zt_bf1")
         nc.scalar.copy(y0_again[:], y_acc0[:])
         y1 = keep.tile([P, HALF], F32, name="y1")
         nc.scalar.copy(y1[:], y_acc1[:])

@@ -1,7 +1,6 @@
 from contextlib import ExitStack
 
 import concourse.mybir as mybir
-from concourse.masks import make_identity
 
 K, T, S, H, N, V = 1024, 1024, 512, 512, 128, 256
 FLOPS = 2 * K * H * S + 2 * H * N * V
@@ -38,38 +37,42 @@ def tile_picked_zunm_none_p_kernel(
         w2s = keep.tile([P, N], U8, name="w2s", align_bytes=64)
         w2c = keep.tile([P, N], I32, name="w2c", align_bytes=64)
         xw_all = [keep.tile([P, T], I32, name="xw_all%d" % g, align_bytes=64) for g in range(PASSES)]
-        w_raw = [[keep.tile([P, PACK, 2 * P], F32, name="w_raw%d%d" % (w, g), align_bytes=64) for g in range(PASSES)] for w in range(2)]
-        ident = keep.tile([P, P], F32, name="ident")
-        gate_sb = [keep.tile([P, HALF], F32, name="gate%d" % c) for c in range(2)]
+        spans = [[(0, PACK)], [(0, 2), (2, PACK)]]
+        w_raw = {
+            (g, lo): keep.tile([P, hi - lo, H], F32, name="w_raw%d%d" % (g, lo), align_bytes=64)
+            for g in range(PASSES)
+            for lo, hi in spans[g]
+        }
+        stage = keep.tile([P, TILES + 2, HALF], F32, name="stage", align_bytes=64)
+        gate1 = keep.tile([P, HALF], F32, name="gate1")
+        gates = [stage[:, 0, :], gate1[:]]
         back_sb = keep.tile([P, V], F32, name="back_sb")
 
         nc.gpsimd.memset(xs_all[:].bitcast(I32), 0)
         nc.gpsimd.memset(w2s[:].bitcast(I32), 0)
-        make_identity(nc, ident[:])
 
         def load_words(g):
             nc.sync.dma_start(xw_all[g][:], x_words[g].rearrange("p n t -> p (n t)").bitcast(I32))
 
-        def load_w(w, g):
+        def load_w(g):
             rows = w1[512 * g : 512 * (g + 1), :].rearrange("(p j) c -> p j c", j=PACK)
-            nc.sync.dma_start(w_raw[w][g][:], rows[:, :, 2 * P * w : 2 * P * (w + 1)])
+            for lo, hi in spans[g]:
+                nc.sync.dma_start(w_raw[g, lo][:], rows[:, lo:hi, :])
 
         nc.sync.dma_start(offs_sb[:], offs)
-        load_w(0, 0)
+        load_words(0)
+        nc.sync.dma_start(kb_sb[:], kb)
         for q in range(4):
             nc.sync.dma_start(
                 xs_all[32 * q : 32 * q + 8, :].bitcast(I32),
                 x_scales[:, 4 * q : 4 * q + 4, :].bitcast(I32),
             )
-        load_words(0)
-        load_w(0, 1)
+        load_w(0)
         load_words(1)
-        nc.sync.dma_start(kb_sb[:], kb)
+        load_w(1)
+        nc.sync.dma_start(gates[0], gate[:, 0:HALF])
+        nc.sync.dma_start(gates[1], gate[:, HALF:V])
         nc.sync.dma_start(ka_sb[:], ka)
-        nc.sync.dma_start(gate_sb[0][:], gate[:, 0:HALF])
-        load_w(1, 0)
-        load_w(1, 1)
-        nc.sync.dma_start(gate_sb[1][:], gate[:, HALF:V])
         nc.sync.dma_start(w2c[:], w2_words[0].rearrange("p n t -> p (n t)").bitcast(I32))
         for q in range(4):
             nc.sync.dma_start(
@@ -78,48 +81,70 @@ def tile_picked_zunm_none_p_kernel(
             )
         nc.sync.dma_start(back_sb[:], back)
 
-        xw = {}
+        xw = [keep.tile([P, S], U32, name="xw%d" % g, align_bytes=64) for g in range(PASSES)]
         xs = keep.tile([P, S], U8, name="xs", align_bytes=64)
         wc, ws = {}, {}
 
-        def gather_words(g, tag):
-            xw[g] = keep.tile([P, S], U32, name="xw%d" % g, tag=tag, align_bytes=64)
+        def gather_words(g):
             nc.vector.tensor_copy(xw[g][:], xw_all[g][:].bitcast(U32).indirect(offs_sb[:]))
 
-        def cast_w(w, g, s_lo, s_hi, engine_copy, tag):
-            w_bf = keep.tile([P, (s_hi - s_lo) * H], BF16, name="w_bf%d%d%d" % (w, g, s_lo), tag=tag, align_bytes=64)
-            engine_copy(
-                w_bf[:].rearrange("p (s q e j) -> p q s j e", q=64, e=2, j=PACK),
-                w_raw[w][g][:].rearrange("p j (q s e) -> p q s j e", s=2, e=2)[:, :, s_lo:s_hi],
-            )
+        def cast_w(g, pair, engine_copy):
+            w_bf = keep.tile([P, 2 * H], BF16, name="w_bf%d%d" % (g, pair), align_bytes=64)
+            for lo, hi in spans[g]:
+                engine_copy(
+                    w_bf[:].rearrange("p (t m j) -> p m j t", t=2, j=PACK)[:, :, lo:hi, :],
+                    w_raw[g, lo][:].rearrange("p j (m t) -> p m j t", t=PACK)[:, :, :, 2 * pair : 2 * pair + 2],
+                )
             return w_bf
 
-        def quantize_w(w, g, s_lo, s_hi, w_bf):
-            width = P * (s_hi - s_lo)
-            codes = keep.tile([P, width], U32, name="wc%d%d%d" % (w, g, s_lo), align_bytes=64)
-            scales = keep.tile([P, width], U8, name="ws%d%d%d" % (w, g, s_lo), align_bytes=64)
-            nc.vector.quantize_mx(out=codes[:].bitcast(FP8X4), scales=scales[:], in_=w_bf[:])
-            for s in range(s_lo, s_hi):
-                wc[w, g, s] = codes[:, P * (s - s_lo) : P * (s - s_lo + 1)]
-                ws[w, g, s] = scales[:, P * (s - s_lo) : P * (s - s_lo + 1)]
+        def quantize_w(g, t_lo, t_hi, w_bf, tag):
+            width = P * (t_hi - t_lo)
+            codes = keep.tile([P, width], U32, name="wc%d%d" % (g, t_lo), tag=tag, align_bytes=64)
+            scales = keep.tile([P, width], U8, name="ws%d%d" % (g, t_lo), align_bytes=64)
+            first = H * (t_lo % 2)
+            nc.vector.quantize_mx(out=codes[:].bitcast(FP8X4), scales=scales[:], in_=w_bf[:, first : first + PACK * width])
+            for t in range(t_lo, t_hi):
+                wc[g, t] = codes[:, P * (t - t_lo) : P * (t - t_lo + 1)]
+                ws[g, t] = scales[:, P * (t - t_lo) : P * (t - t_lo + 1)]
 
-        h = []
+        acc = [None] + [psum.tile([P, S], F32, name="acc%d" % t, tag="bank%d" % t) for t in range(1, TILES)]
+        acc0 = [psum.tile([P, S // 2], F32, name="acc0%d" % c, tag="bank0%d" % c) for c in range(2)]
+        h = [keep.tile([P, S], F32, name="h%d" % t, align_bytes=64) for t in range(TILES)]
 
-        def product(w, s, tag):
-            u = 2 * w + s
-            acc = psum.tile([P, S], F32, name="acc%d" % u, tag="bank%d" % u)
-            for g in range(PASSES):
-                nc.tensor.matmul_mx(
-                    out=acc[:],
-                    lhsT=wc[w, g, s].bitcast(FP8X4),
-                    lhsT_scale=ws[w, g, s],
-                    rhs=xw[g][:].bitcast(FP8X4),
-                    rhs_scale=xs[4 * g : P, :],
-                    start=(g == 0),
-                    stop=(g == PASSES - 1),
-                )
-            h.append(keep.tile([P, S], F32, name="h%d" % u, tag=tag, align_bytes=64))
-            nc.scalar.copy(h[u][:], acc[:])
+        def product(g, t, bank, lo, hi):
+            nc.tensor.matmul_mx(
+                out=bank[:],
+                lhsT=wc[g, t].bitcast(FP8X4),
+                lhsT_scale=ws[g, t],
+                rhs=xw[g][:, lo:hi].bitcast(FP8X4),
+                rhs_scale=xs[4 * g : P, lo:hi],
+                start=(g == 0),
+                stop=(g == PASSES - 1),
+            )
+
+        gather_words(0)
+        nc.vector.tensor_copy(xs[:], xs_all[:].indirect(offs_sb[:]))
+        by_vector = cast_w(0, 0, nc.vector.tensor_copy)
+        by_scalar = cast_w(0, 1, nc.scalar.copy)
+        quantize_w(0, 0, 2, by_vector, "wc00")
+        quantize_w(0, 2, 4, by_scalar, "wc02")
+        product(0, 0, acc0[0], 0, S // 2)
+        product(0, 0, acc0[1], S // 2, S)
+        for t in range(1, TILES):
+            product(0, t, acc[t], 0, S)
+        gather_words(1)
+        by_vector = cast_w(1, 0, nc.vector.tensor_copy)
+        by_scalar = cast_w(1, 1, nc.scalar.copy)
+        quantize_w(1, 0, 1, by_vector, "wc10")
+        quantize_w(1, 1, 2, by_vector, "wc11")
+        product(1, 0, acc0[0], 0, S // 2)
+        product(1, 0, acc0[1], S // 2, S)
+        nc.vector.tensor_copy(h[0][:, 0 : S // 2], acc0[0][:])
+        nc.scalar.copy(h[0][:, S // 2 : S], acc0[1][:])
+        quantize_w(1, 2, 4, by_scalar, "wc10")
+        for t in range(1, TILES):
+            product(1, t, acc[t], 0, S)
+            nc.scalar.copy(h[t][:], acc[t][:])
 
         window = keep.tile([P, S], F32, name="window")
         cols = HALF // 16
@@ -127,32 +152,29 @@ def tile_picked_zunm_none_p_kernel(
         def entries(list_sb, c):
             return list_sb[:, c * cols : (c + 1) * cols]
 
-        def look_up(c, u, pair):
-            nc.vector.tensor_tensor(pair[:, 0, :], h[u][:].indirect(entries(kb_sb, c)), gate_sb[c][:], MULT)
-            nc.vector.tensor_copy(pair[:, 1, :], h[u][:].indirect(entries(ka_sb, c)))
+        spare = keep.tile([P, 2 * TILES - 1, HALF], F32, name="spare")
+        gated = [[spare[:, 0, :], spare[:, 1, :], spare[:, 2, :], stage[:, 1, :]], [spare[:, 3 + t, :] for t in range(TILES)]]
+        z = [stage[:, 2 : 2 + TILES, :], stage[:, 0:TILES, :]]
 
-        def turn_and_add(zt, pair):
-            for i in range(2):
-                nc.tensor.matmul(zt, pair[:, i, :], ident[:], is_transpose=True, start=(i == 0), stop=(i == 1))
+        def second_member(c, t):
+            nc.vector.tensor_tensor(gated[c][t], h[t][:].indirect(entries(kb_sb, c)), gates[c], MULT)
 
-        def second_product(c, pairs, bank):
-            zt_bf = keep.tile([P, H], BF16, name="zt_bf%d" % c)
-            for lo, hi, zt_bank in ((0, 3, "bank%d" % (4 + c)), (3, 4, "bank%d" % (5 - c))):
-                zt = psum.tile([P, P * (hi - lo)], F32, name="zt%d_%d" % (c, lo), tag=zt_bank)
-                for u in range(lo, hi):
-                    block = 2 * (u % 2) + u // 2 - lo
-                    turn_and_add(zt[:, P * block : P * (block + 1)], pairs[:, u])
-                nc.scalar.copy(zt_bf[:, P * lo : P * hi], zt[:])
-            words = zt_bf[:].bitcast(F32)
-            turned = psum.tile([P, 2, HALF], F32, name="turned%d" % c, tag="bank6")
-            for r in range(2):
-                nc.tensor.transpose(turned[:, r, :], words[:, P * r : P * (r + 1)], ident[:])
-            z_bf = keep.tile([P, HALF * PACK], BF16, name="z_bf%d" % c, align_bytes=64)
-            nc.scalar.copy(z_bf[:].bitcast(F32).rearrange("p (v r) -> p v r", r=2), turned[:].rearrange("p r v -> p v r"))
+        def first_member(c, t):
+            nc.vector.tensor_tensor(z[c][:, t, :], h[t][:].indirect(entries(ka_sb, c)), gated[c][t], ADD)
+
+        def interleave(c, tag):
+            z_bf = keep.tile([P, HALF * PACK], BF16, name="z_bf%d" % c, tag=tag, align_bytes=64)
+            nc.scalar.copy(
+                z_bf[:].rearrange("p (v i t) -> p v t i", i=4, t=PACK),
+                z[c].rearrange("p t (v i) -> p v t i", i=4),
+            )
+            return z_bf
+
+        def second_product(c, z_bf):
             zc = keep.tile([P, HALF], U32, name="zc%d" % c, align_bytes=64)
             zs = keep.tile([P, HALF], U8, name="zs%d" % c, align_bytes=64)
             nc.vector.quantize_mx(out=zc[:].bitcast(FP8X4), scales=zs[:], in_=z_bf[:])
-            y_acc = psum.tile([P, HALF], F32, name="y_acc%d" % c, tag=bank)
+            y_acc = psum.tile([P, HALF], F32, name="y_acc%d" % c, tag="bank%d" % (TILES + c))
             nc.tensor.matmul_mx(
                 out=y_acc[:],
                 lhsT=w2c[:].bitcast(FP8X4),
@@ -164,41 +186,26 @@ def tile_picked_zunm_none_p_kernel(
             )
             return y_acc
 
-
-        nc.vector.tensor_copy(xs[:], xs_all[:].indirect(offs_sb[:]))
-        gather_words(0, "xw0")
-        quantize_w(0, 0, 0, 2, cast_w(0, 0, 0, 2, nc.scalar.copy, "w_bf000"))
-        quantize_w(0, 1, 0, 1, cast_w(0, 1, 0, 1, nc.scalar.copy, "w_bf010"))
-        gather_words(1, "w_bf010")
-        quantize_w(0, 1, 1, 2, cast_w(0, 1, 1, 2, nc.scalar.copy, "w_bf011"))
-        by_scalar = cast_w(1, 0, 1, 2, nc.scalar.copy, "w_bf101")
-        by_vector = cast_w(1, 0, 0, 1, nc.vector.tensor_copy, "w_raw01")
-        quantize_w(1, 0, 0, 1, by_vector)
-        quantize_w(1, 0, 1, 2, by_scalar)
-        product(0, 0, "w_raw10")
-        by_scalar = cast_w(1, 1, 1, 2, nc.scalar.copy, "wc010")
-        by_vector = cast_w(1, 1, 0, 1, nc.vector.tensor_copy, "w_raw01")
-        quantize_w(1, 1, 0, 1, by_vector)
-        quantize_w(1, 1, 1, 2, by_scalar)
-        product(0, 1, "w_raw11")
-        product(1, 0, "h2")
-        product(1, 1, "h3")
-        first = keep.tile([P, TILES, 2, HALF], F32, name="first", tag="w_raw01", align_bytes=64)
-        for u in range(TILES):
-            look_up(0, u, first[:, u])
-        second = keep.tile([P, TILES, 2, HALF], F32, name="second", tag="gate0")
-        for u in range(TILES):
-            look_up(1, u, second[:, u])
-        y_acc0 = second_product(0, first, "bank7")
+        for t in range(TILES):
+            second_member(0, t)
+            second_member(1, t)
+            first_member(0, t)
+        z_bf = interleave(0, "z_bf0")
+        first_member(1, 0)
+        first_member(1, 1)
+        y_acc0 = second_product(0, z_bf)
         y0 = keep.tile([P, HALF], F32, name="y0")
         nc.scalar.copy(y0[:], y_acc0[:])
-        y_acc1 = second_product(1, second, "bank1")
-        y0_again = keep.tile([P, HALF], F32, name="y0_again", tag="zt_bf1")
-        nc.scalar.copy(y0_again[:], y_acc0[:])
+        first_member(1, 2)
+        first_member(1, 3)
+        z_bf = interleave(1, "zc0")
+        nc.vector.tensor_copy(window[:].indirect(entries(ka_sb, 0)), y0[:])
+        y_acc1 = second_product(1, z_bf)
+        y0_again = stage[:, 0, :]
+        nc.scalar.copy(y0_again, y_acc0[:])
         y1 = keep.tile([P, HALF], F32, name="y1")
         nc.scalar.copy(y1[:], y_acc1[:])
-        nc.vector.tensor_copy(window[:].indirect(entries(ka_sb, 0)), y0[:])
-        nc.vector.tensor_tensor(window[:].indirect(entries(kb_sb, 0)), y0_again[:], back_sb[:, 0:HALF], MULT)
+        nc.vector.tensor_tensor(window[:].indirect(entries(kb_sb, 0)), y0_again, back_sb[:, 0:HALF], MULT)
         nc.vector.tensor_copy(window[:].indirect(entries(ka_sb, 1)), y1[:])
         nc.vector.tensor_tensor(window[:].indirect(entries(kb_sb, 1)), y1[:], back_sb[:, HALF:V], MULT)
         nc.sync.dma_start(out, window[:])

@@ -54,22 +54,23 @@ def tile_picked_zunm_none_p_kernel(
         def load_words(g):
             nc.sync.dma_start(xw_all[g][:], x_words[g].rearrange("p n t -> p (n t)").bitcast(I32))
 
-        def load_w(g):
+        def load_w(g, half, dst):
             rows = w1[512 * g : 512 * (g + 1), :].rearrange("(p j) c -> p j c", j=PACK)
-            for lo, hi in spans[g]:
-                nc.sync.dma_start(w_raw[g, lo][:], rows[:, lo:hi, :])
+            nc.sync.dma_start(dst, rows[:, 2 * half : 2 * half + 2, :])
 
-        nc.sync.dma_start(offs_sb[:], offs)
         load_words(0)
-        nc.sync.dma_start(kb_sb[:], kb)
+        nc.sync.dma_start(offs_sb[:], offs)
+        load_w(0, 0, w_raw[0, 0][:, 0:2, :])
         for q in range(4):
             nc.sync.dma_start(
                 xs_all[32 * q : 32 * q + 8, :].bitcast(I32),
                 x_scales[:, 4 * q : 4 * q + 4, :].bitcast(I32),
             )
-        load_w(0)
+        load_w(0, 1, w_raw[0, 0][:, 2:4, :])
         load_words(1)
-        load_w(1)
+        load_w(1, 0, w_raw[1, 0][:])
+        load_w(1, 1, w_raw[1, 2][:])
+        nc.sync.dma_start(kb_sb[:], kb)
         nc.sync.dma_start(gates[0], gate[:, 0:HALF])
         nc.sync.dma_start(gates[1], gate[:, HALF:V])
         nc.sync.dma_start(ka_sb[:], ka)
@@ -88,21 +89,30 @@ def tile_picked_zunm_none_p_kernel(
         def gather_words(g):
             nc.vector.tensor_copy(xw[g][:], xw_all[g][:].bitcast(U32).indirect(offs_sb[:]))
 
-        def cast_w(g, pair, engine_copy):
-            w_bf = keep.tile([P, 2 * H], BF16, name="w_bf%d%d" % (g, pair), align_bytes=64)
-            for lo, hi in spans[g]:
-                engine_copy(
-                    w_bf[:].rearrange("p (t m j) -> p m j t", t=2, j=PACK)[:, :, lo:hi, :],
-                    w_raw[g, lo][:].rearrange("p j (m t) -> p m j t", t=PACK)[:, :, :, 2 * pair : 2 * pair + 2],
-                )
-            return w_bf
+        w_bf = {
+            (g, pair): keep.tile([P, 2 * H], BF16, name="w_bf%d%d" % (g, pair), align_bytes=64)
+            for g in range(PASSES)
+            for pair in range(2)
+        }
 
-        def quantize_w(g, t_lo, t_hi, w_bf, tag):
+        def cast_w(engine_copy, g, rows, tiles, places=(0, P)):
+            first = rows[0] if g == 1 else 0
+            pair = tiles[0] // 2
+            engine_copy(
+                w_bf[g, pair][:].rearrange("p (t m j) -> p m j t", t=2, j=PACK)[
+                    :, places[0] : places[1], rows[0] : rows[1], tiles[0] - 2 * pair : tiles[1] - 2 * pair
+                ],
+                w_raw[g, first][:].rearrange("p j (m t) -> p m j t", t=PACK)[
+                    :, places[0] : places[1], rows[0] - first : rows[1] - first, tiles[0] : tiles[1]
+                ],
+            )
+
+        def quantize_w(g, t_lo, t_hi, tag):
             width = P * (t_hi - t_lo)
             codes = keep.tile([P, width], U32, name="wc%d%d" % (g, t_lo), tag=tag, align_bytes=64)
             scales = keep.tile([P, width], U8, name="ws%d%d" % (g, t_lo), align_bytes=64)
             first = H * (t_lo % 2)
-            nc.vector.quantize_mx(out=codes[:].bitcast(FP8X4), scales=scales[:], in_=w_bf[:, first : first + PACK * width])
+            nc.vector.quantize_mx(out=codes[:].bitcast(FP8X4), scales=scales[:], in_=w_bf[g, t_lo // 2][:, first : first + PACK * width])
             for t in range(t_lo, t_hi):
                 wc[g, t] = codes[:, P * (t - t_lo) : P * (t - t_lo + 1)]
                 ws[g, t] = scales[:, P * (t - t_lo) : P * (t - t_lo + 1)]
@@ -124,24 +134,29 @@ def tile_picked_zunm_none_p_kernel(
 
         gather_words(0)
         nc.vector.tensor_copy(xs[:], xs_all[:].indirect(offs_sb[:]))
-        by_vector = cast_w(0, 0, nc.vector.tensor_copy)
-        by_scalar = cast_w(0, 1, nc.scalar.copy)
-        quantize_w(0, 0, 2, by_vector, "wc00")
-        quantize_w(0, 2, 4, by_scalar, "wc02")
+        cast_w(nc.scalar.copy, 0, (0, 2), (2, 4))
+        cast_w(nc.vector.tensor_copy, 0, (0, 4), (0, 2))
+        cast_w(nc.scalar.copy, 0, (2, 4), (2, 4))
+        quantize_w(0, 0, 2, "wc00")
+        quantize_w(0, 2, 4, "wc02")
         product(0, 0, acc0[0], 0, S // 2)
         product(0, 0, acc0[1], S // 2, S)
         for t in range(1, TILES):
             product(0, t, acc[t], 0, S)
         gather_words(1)
-        by_vector = cast_w(1, 0, nc.vector.tensor_copy)
-        by_scalar = cast_w(1, 1, nc.scalar.copy)
-        quantize_w(1, 0, 1, by_vector, "wc10")
-        quantize_w(1, 1, 2, by_vector, "wc11")
+        cast_w(nc.vector.tensor_copy, 1, (0, 2), (0, 2))
+        cast_w(nc.scalar.copy, 1, (0, 2), (2, 4))
+        cast_w(nc.vector.tensor_copy, 1, (2, 4), (0, 1), (0, P // 2))
+        cast_w(nc.scalar.copy, 1, (2, 4), (0, 1), (P // 2, P))
+        cast_w(nc.vector.tensor_copy, 1, (2, 4), (1, 2))
+        cast_w(nc.scalar.copy, 1, (2, 4), (2, 4))
+        quantize_w(1, 0, 1, "wc10")
+        quantize_w(1, 1, 2, "wc11")
         product(1, 0, acc0[0], 0, S // 2)
         product(1, 0, acc0[1], S // 2, S)
         nc.vector.tensor_copy(h[0][:, 0 : S // 2], acc0[0][:])
         nc.scalar.copy(h[0][:, S // 2 : S], acc0[1][:])
-        quantize_w(1, 2, 4, by_scalar, "wc10")
+        quantize_w(1, 2, 4, "wc10")
         for t in range(1, TILES):
             product(1, t, acc[t], 0, S)
             nc.scalar.copy(h[t][:], acc[t][:])
@@ -154,21 +169,20 @@ def tile_picked_zunm_none_p_kernel(
 
         spare = keep.tile([P, 2 * TILES - 1, HALF], F32, name="spare")
         gated = [[spare[:, 0, :], spare[:, 1, :], spare[:, 2, :], stage[:, 1, :]], [spare[:, 3 + t, :] for t in range(TILES)]]
-        z = [stage[:, 2 : 2 + TILES, :], stage[:, 0:TILES, :]]
+        slots = [[4, 5, 2, 3], [0, 1, 2, 3]]
 
         def second_member(c, t):
             nc.vector.tensor_tensor(gated[c][t], h[t][:].indirect(entries(kb_sb, c)), gates[c], MULT)
 
         def first_member(c, t):
-            nc.vector.tensor_tensor(z[c][:, t, :], h[t][:].indirect(entries(ka_sb, c)), gated[c][t], ADD)
+            nc.vector.tensor_tensor(stage[:, slots[c][t], :], h[t][:].indirect(entries(ka_sb, c)), gated[c][t], ADD)
 
-        def interleave(c, tag):
-            z_bf = keep.tile([P, HALF * PACK], BF16, name="z_bf%d" % c, tag=tag, align_bytes=64)
+        def interleave(c, z_bf, lo, hi):
+            first = slots[c][lo]
             nc.scalar.copy(
-                z_bf[:].rearrange("p (v i t) -> p v t i", i=4, t=PACK),
-                z[c].rearrange("p t (v i) -> p v t i", i=4),
+                z_bf[:].rearrange("p (v i t) -> p v t i", i=4, t=PACK)[:, :, lo:hi, :],
+                stage[:, first : first + hi - lo, :].rearrange("p t (v i) -> p v t i", i=4),
             )
-            return z_bf
 
         def second_product(c, z_bf):
             zc = keep.tile([P, HALF], U32, name="zc%d" % c, align_bytes=64)
@@ -190,7 +204,9 @@ def tile_picked_zunm_none_p_kernel(
             second_member(0, t)
             second_member(1, t)
             first_member(0, t)
-        z_bf = interleave(0, "z_bf0")
+        z_bf = keep.tile([P, HALF * PACK], BF16, name="z_bf0", align_bytes=64)
+        interleave(0, z_bf, 0, 2)
+        interleave(0, z_bf, 2, 4)
         first_member(1, 0)
         first_member(1, 1)
         y_acc0 = second_product(0, z_bf)
@@ -198,7 +214,8 @@ def tile_picked_zunm_none_p_kernel(
         nc.scalar.copy(y0[:], y_acc0[:])
         first_member(1, 2)
         first_member(1, 3)
-        z_bf = interleave(1, "zc0")
+        z_bf = keep.tile([P, HALF * PACK], BF16, name="z_bf1", tag="zc0", align_bytes=64)
+        interleave(1, z_bf, 0, 4)
         nc.vector.tensor_copy(window[:].indirect(entries(ka_sb, 0)), y0[:])
         y_acc1 = second_product(1, z_bf)
         y0_again = stage[:, 0, :]

@@ -48,8 +48,8 @@ def tile_picked_zunm_none_p_kernel(
         gates = [stage[:, 0, :], gate1[:]]
         back_sb = keep.tile([P, V], F32, name="back_sb")
 
-        nc.gpsimd.memset(xs_all[:].bitcast(I32), 0)
-        nc.gpsimd.memset(w2s[:].bitcast(I32), 0)
+        nc.vector.memset(xs_all[:].bitcast(I32), 0)
+        nc.vector.memset(w2s[:].bitcast(I32), 0)
 
         def load_words(g):
             nc.sync.dma_start(xw_all[g][:], x_words[g].rearrange("p n t -> p (n t)").bitcast(I32))

@@ -43,9 +43,9 @@ def tile_picked_zunm_none_p_kernel(
             for g in range(PASSES)
             for lo, hi in spans[g]
         }
-        stage = keep.tile([P, TILES + 2, HALF], F32, name="stage", align_bytes=64)
-        gate1 = keep.tile([P, HALF], F32, name="gate1")
-        gates = [stage[:, 0, :], gate1[:]]
+        work = keep.tile([P, 10, HALF], F32, name="work", align_bytes=64)
+        gate_sb = [keep.tile([P, HALF], F32, name="gate%d" % c) for c in range(2)]
+        gates = [tile[:] for tile in gate_sb]
         back_sb = keep.tile([P, V], F32, name="back_sb")
 
         nc.vector.memset(xs_all[:].bitcast(I32), 0)
@@ -159,7 +159,10 @@ def tile_picked_zunm_none_p_kernel(
         quantize_w(1, 2, 4, "wc10")
         for t in range(1, TILES):
             product(1, t, acc[t], 0, S)
-            nc.scalar.copy(h[t][:], acc[t][:])
+        nc.scalar.copy(h[1][:], acc[1][:])
+        for lo, hi in ((0, 384), (384, S)):
+            for t in (2, 3):
+                nc.scalar.copy(h[t][:, lo:hi], acc[t][:, lo:hi])
 
         window = keep.tile([P, S], F32, name="window")
         cols = HALF // 16
@@ -167,21 +170,19 @@ def tile_picked_zunm_none_p_kernel(
         def entries(list_sb, c):
             return list_sb[:, c * cols : (c + 1) * cols]
 
-        spare = keep.tile([P, 2 * TILES - 1, HALF], F32, name="spare")
-        gated = [[spare[:, 0, :], spare[:, 1, :], spare[:, 2, :], stage[:, 1, :]], [spare[:, 3 + t, :] for t in range(TILES)]]
-        slots = [[4, 5, 2, 3], [0, 1, 2, 3]]
+        gated_at = [[0, 1, 2, 3], [8, 9, 8, 7]]
+        z_at = [4, 2]
 
         def second_member(c, t):
-            nc.vector.tensor_tensor(gated[c][t], h[t][:].indirect(entries(kb_sb, c)), gates[c], MULT)
+            nc.vector.tensor_tensor(work[:, gated_at[c][t], :], h[t][:].indirect(entries(kb_sb, c)), gates[c], MULT)
 
         def first_member(c, t):
-            nc.vector.tensor_tensor(stage[:, slots[c][t], :], h[t][:].indirect(entries(ka_sb, c)), gated[c][t], ADD)
+            nc.vector.tensor_tensor(work[:, z_at[c] + t, :], h[t][:].indirect(entries(ka_sb, c)), work[:, gated_at[c][t], :], ADD)
 
         def interleave(c, z_bf, lo, hi):
-            first = slots[c][lo]
             nc.scalar.copy(
                 z_bf[:].rearrange("p (v i t) -> p v t i", i=4, t=PACK)[:, :, lo:hi, :],
-                stage[:, first : first + hi - lo, :].rearrange("p t (v i) -> p v t i", i=4),
+                work[:, z_at[c] + lo : z_at[c] + hi, :].rearrange("p t (v i) -> p v t i", i=4),
             )
 
         def second_product(c, z_bf):
@@ -200,29 +201,37 @@ def tile_picked_zunm_none_p_kernel(
             )
             return y_acc
 
-        for t in range(TILES):
+        for t in range(2):
             second_member(0, t)
             second_member(1, t)
             first_member(0, t)
+        second_member(0, 2)
+        second_member(0, 3)
+        first_member(0, 2)
+        first_member(0, 3)
         z_bf = keep.tile([P, HALF * PACK], BF16, name="z_bf0", align_bytes=64)
         interleave(0, z_bf, 0, 2)
         interleave(0, z_bf, 2, 4)
         first_member(1, 0)
         first_member(1, 1)
+        second_member(1, 2)
         y_acc0 = second_product(0, z_bf)
         y0 = keep.tile([P, HALF], F32, name="y0")
         nc.scalar.copy(y0[:], y_acc0[:])
+        second_member(1, 3)
         first_member(1, 2)
         first_member(1, 3)
         z_bf = keep.tile([P, HALF * PACK], BF16, name="z_bf1", tag="zc0", align_bytes=64)
         interleave(1, z_bf, 0, 4)
         nc.vector.tensor_copy(window[:].indirect(entries(ka_sb, 0)), y0[:])
         y_acc1 = second_product(1, z_bf)
-        y0_again = stage[:, 0, :]
+        y0_again = work[:, z_at[1], :]
         nc.scalar.copy(y0_again, y_acc0[:])
         y1 = keep.tile([P, HALF], F32, name="y1")
         nc.scalar.copy(y1[:], y_acc1[:])
         nc.vector.tensor_tensor(window[:].indirect(entries(kb_sb, 0)), y0_again, back_sb[:, 0:HALF], MULT)
+        y1b = keep.tile([P, HALF], F32, name="y1b")
+        nc.vector.tensor_tensor(y1b[:], y_acc1[:], back_sb[:, HALF:V], MULT)
         nc.vector.tensor_copy(window[:].indirect(entries(ka_sb, 1)), y1[:])
-        nc.vector.tensor_tensor(window[:].indirect(entries(kb_sb, 1)), y1[:], back_sb[:, HALF:V], MULT)
+        nc.vector.tensor_copy(window[:].indirect(entries(kb_sb, 1)), y1b[:])
         nc.sync.dma_start(out, window[:])

@@ -176,13 +176,14 @@ def tile_picked_zunm_none_p_kernel(
         def second_member(c, t):
             nc.vector.tensor_tensor(work[:, gated_at[c][t], :], h[t][:].indirect(entries(kb_sb, c)), gates[c], MULT)
 
-        def first_member(c, t):
-            nc.vector.tensor_tensor(work[:, z_at[c] + t, :], h[t][:].indirect(entries(ka_sb, c)), work[:, gated_at[c][t], :], ADD)
+        def first_member(c, t, lo=0, hi=HALF):
+            offsets = ka_sb[:, (c * HALF + lo) // 16 : (c * HALF + hi) // 16]
+            nc.vector.tensor_tensor(work[:, z_at[c] + t, lo:hi], h[t][:].indirect(offsets), work[:, gated_at[c][t], lo:hi], ADD)
 
-        def interleave(c, z_bf, lo, hi):
+        def interleave(c, z_bf, lo, hi, first=0, last=HALF):
             nc.scalar.copy(
-                z_bf[:].rearrange("p (v i t) -> p v t i", i=4, t=PACK)[:, :, lo:hi, :],
-                work[:, z_at[c] + lo : z_at[c] + hi, :].rearrange("p t (v i) -> p v t i", i=4),
+                z_bf[:, PACK * first : PACK * last].rearrange("p (v i t) -> p v t i", i=4, t=PACK)[:, :, lo:hi, :],
+                work[:, z_at[c] + lo : z_at[c] + hi, first:last].rearrange("p t (v i) -> p v t i", i=4),
             )
 
         def second_product(c, z_bf):
@@ -219,10 +220,11 @@ def tile_picked_zunm_none_p_kernel(
         y0 = keep.tile([P, HALF], F32, name="y0")
         nc.scalar.copy(y0[:], y_acc0[:])
         second_member(1, 3)
-        first_member(1, 2)
-        first_member(1, 3)
         z_bf = keep.tile([P, HALF * PACK], BF16, name="z_bf1", tag="zc0", align_bytes=64)
-        interleave(1, z_bf, 0, 4)
+        for first in (0, HALF // 2):
+            first_member(1, 2, first, first + HALF // 2)
+            first_member(1, 3, first, first + HALF // 2)
+            interleave(1, z_bf, 0, 4, first, first + HALF // 2)
         nc.vector.tensor_copy(window[:].indirect(entries(ka_sb, 0)), y0[:])
         y_acc1 = second_product(1, z_bf)
         y0_again = work[:, z_at[1], :]

@@ -14,6 +14,7 @@ U8 = mybir.dt.uint8
 FP8X4 = mybir.dt.float8_e4m3fn_x4
 MULT = mybir.AluOpType.mult
 ADD = mybir.AluOpType.add
+COPY = mybir.ActivationFunctionType.Copy
 
 P = 128
 PACK = 4
@@ -37,42 +38,42 @@ def tile_picked_zunm_none_p_kernel(
         w2s = keep.tile([P, N], U8, name="w2s", align_bytes=64)
         w2c = keep.tile([P, N], I32, name="w2c", align_bytes=64)
         xw_all = [keep.tile([P, T], I32, name="xw_all%d" % g, align_bytes=64) for g in range(PASSES)]
-        spans = [[(0, PACK)], [(0, 2), (2, PACK)]]
         w_raw = {
-            (g, lo): keep.tile([P, hi - lo, H], F32, name="w_raw%d%d" % (g, lo), align_bytes=64)
+            (g, half): keep.tile([P, 2, H], F32, name="w_raw%d%d" % (g, half), align_bytes=64)
             for g in range(PASSES)
-            for lo, hi in spans[g]
+            for half in range(2)
         }
-        work = keep.tile([P, 10, HALF], F32, name="work", align_bytes=64)
-        gate_sb = [keep.tile([P, HALF], F32, name="gate%d" % c) for c in range(2)]
-        gates = [tile[:] for tile in gate_sb]
-        back_sb = keep.tile([P, V], F32, name="back_sb")
+        gate_sb = keep.tile([P, V], F32, name="gate_sb", align_bytes=64)
+        back_sb = keep.tile([P, V], F32, name="back_sb", align_bytes=64)
+        first_win = keep.tile([P, S], F32, name="first_win", align_bytes=64)
+        second_win = keep.tile([P, S], F32, name="second_win", align_bytes=64)
 
         nc.vector.memset(xs_all[:].bitcast(I32), 0)
         nc.vector.memset(w2s[:].bitcast(I32), 0)
+        nc.vector.memset(first_win[:], 0.0)
+        nc.vector.memset(second_win[:], 0.0)
 
         def load_words(g):
             nc.sync.dma_start(xw_all[g][:], x_words[g].rearrange("p n t -> p (n t)").bitcast(I32))
 
-        def load_w(g, half, dst):
+        def load_w(g, half):
             rows = w1[512 * g : 512 * (g + 1), :].rearrange("(p j) c -> p j c", j=PACK)
-            nc.sync.dma_start(dst, rows[:, 2 * half : 2 * half + 2, :])
+            nc.sync.dma_start(w_raw[g, half][:], rows[:, 2 * half : 2 * half + 2, :])
 
         load_words(0)
         nc.sync.dma_start(offs_sb[:], offs)
-        load_w(0, 0, w_raw[0, 0][:, 0:2, :])
+        load_w(0, 0)
         for q in range(4):
             nc.sync.dma_start(
                 xs_all[32 * q : 32 * q + 8, :].bitcast(I32),
                 x_scales[:, 4 * q : 4 * q + 4, :].bitcast(I32),
             )
-        load_w(0, 1, w_raw[0, 0][:, 2:4, :])
+        load_w(0, 1)
         load_words(1)
-        load_w(1, 0, w_raw[1, 0][:])
-        load_w(1, 1, w_raw[1, 2][:])
+        load_w(1, 0)
+        load_w(1, 1)
         nc.sync.dma_start(kb_sb[:], kb)
-        nc.sync.dma_start(gates[0], gate[:, 0:HALF])
-        nc.sync.dma_start(gates[1], gate[:, HALF:V])
+        nc.sync.dma_start(gate_sb[:], gate)
         nc.sync.dma_start(ka_sb[:], ka)
         nc.sync.dma_start(w2c[:], w2_words[0].rearrange("p n t -> p (n t)").bitcast(I32))
         for q in range(4):
@@ -84,113 +85,115 @@ def tile_picked_zunm_none_p_kernel(
 
         xw = [keep.tile([P, S], U32, name="xw%d" % g, align_bytes=64) for g in range(PASSES)]
         xs = keep.tile([P, S], U8, name="xs", align_bytes=64)
-        wc, ws = {}, {}
-
-        def gather_words(g):
-            nc.vector.tensor_copy(xw[g][:], xw_all[g][:].bitcast(U32).indirect(offs_sb[:]))
-
         w_bf = {
             (g, pair): keep.tile([P, 2 * H], BF16, name="w_bf%d%d" % (g, pair), align_bytes=64)
             for g in range(PASSES)
             for pair in range(2)
         }
+        wc, ws = {}, {}
 
-        def cast_w(engine_copy, g, rows, tiles, places=(0, P)):
-            first = rows[0] if g == 1 else 0
-            pair = tiles[0] // 2
+        def gather_words(g):
+            nc.vector.tensor_copy(xw[g][:], xw_all[g][:].bitcast(U32).indirect(offs_sb[:]))
+
+        def round_w(engine_copy, g, half, pair):
             engine_copy(
-                w_bf[g, pair][:].rearrange("p (t m j) -> p m j t", t=2, j=PACK)[
-                    :, places[0] : places[1], rows[0] : rows[1], tiles[0] - 2 * pair : tiles[1] - 2 * pair
-                ],
-                w_raw[g, first][:].rearrange("p j (m t) -> p m j t", t=PACK)[
-                    :, places[0] : places[1], rows[0] - first : rows[1] - first, tiles[0] : tiles[1]
-                ],
+                w_bf[g, pair][:].rearrange("p (t m j) -> p m j t", t=2, j=PACK)[:, :, 2 * half : 2 * half + 2, :],
+                w_raw[g, half][:].rearrange("p j (m t) -> p m j t", t=PACK)[:, :, :, 2 * pair : 2 * pair + 2],
             )
 
-        def quantize_w(g, t_lo, t_hi, tag):
+        def quantize_w(g, t_lo, t_hi):
             width = P * (t_hi - t_lo)
-            codes = keep.tile([P, width], U32, name="wc%d%d" % (g, t_lo), tag=tag, align_bytes=64)
+            codes = keep.tile([P, width], U32, name="wc%d%d" % (g, t_lo), tag="wc%d%d" % (g, t_lo), align_bytes=64)
             scales = keep.tile([P, width], U8, name="ws%d%d" % (g, t_lo), align_bytes=64)
             first = H * (t_lo % 2)
-            nc.vector.quantize_mx(out=codes[:].bitcast(FP8X4), scales=scales[:], in_=w_bf[g, t_lo // 2][:, first : first + PACK * width])
+            nc.vector.quantize_mx(
+                out=codes[:].bitcast(FP8X4), scales=scales[:], in_=w_bf[g, t_lo // 2][:, first : first + PACK * width]
+            )
             for t in range(t_lo, t_hi):
                 wc[g, t] = codes[:, P * (t - t_lo) : P * (t - t_lo + 1)]
                 ws[g, t] = scales[:, P * (t - t_lo) : P * (t - t_lo + 1)]
 
-        acc = [None] + [psum.tile([P, S], F32, name="acc%d" % t, tag="bank%d" % t) for t in range(1, TILES)]
-        acc0 = [psum.tile([P, S // 2], F32, name="acc0%d" % c, tag="bank0%d" % c) for c in range(2)]
+        cuts = [[(0, S // 2), (S // 2, S)], [(0, S // 2), (S // 2, S)], [(0, S)], [(0, S)]]
+        acc = {
+            (t, lo): psum.tile([P, hi - lo], F32, name="acc%d_%d" % (t, lo), tag="bank%d_%d" % (t, lo))
+            for t in range(TILES)
+            for lo, hi in cuts[t]
+        }
         h = [keep.tile([P, S], F32, name="h%d" % t, align_bytes=64) for t in range(TILES)]
 
-        def product(g, t, bank, lo, hi):
-            nc.tensor.matmul_mx(
-                out=bank[:],
-                lhsT=wc[g, t].bitcast(FP8X4),
-                lhsT_scale=ws[g, t],
-                rhs=xw[g][:, lo:hi].bitcast(FP8X4),
-                rhs_scale=xs[4 * g : P, lo:hi],
-                start=(g == 0),
-                stop=(g == PASSES - 1),
-            )
+        def product(g, t):
+            for lo, hi in cuts[t]:
+                nc.tensor.matmul_mx(
+                    out=acc[t, lo][:],
+                    lhsT=wc[g, t].bitcast(FP8X4),
+                    lhsT_scale=ws[g, t],
+                    rhs=xw[g][:, lo:hi].bitcast(FP8X4),
+                    rhs_scale=xs[4 * g : P, lo:hi],
+                    start=(g == 0),
+                    stop=(g == PASSES - 1),
+                )
 
         gather_words(0)
         nc.vector.tensor_copy(xs[:], xs_all[:].indirect(offs_sb[:]))
-        cast_w(nc.scalar.copy, 0, (0, 2), (2, 4))
-        cast_w(nc.vector.tensor_copy, 0, (0, 4), (0, 2))
-        cast_w(nc.scalar.copy, 0, (2, 4), (2, 4))
-        quantize_w(0, 0, 2, "wc00")
-        quantize_w(0, 2, 4, "wc02")
-        product(0, 0, acc0[0], 0, S // 2)
-        product(0, 0, acc0[1], S // 2, S)
-        for t in range(1, TILES):
-            product(0, t, acc[t], 0, S)
+        round_w(nc.vector.tensor_copy, 0, 0, 0)
+        round_w(nc.scalar.copy, 0, 0, 1)
+        round_w(nc.vector.tensor_copy, 0, 1, 0)
+        round_w(nc.scalar.copy, 0, 1, 1)
+        quantize_w(0, 0, 2)
+        quantize_w(0, 2, 4)
+        for t in range(TILES):
+            product(0, t)
         gather_words(1)
-        cast_w(nc.vector.tensor_copy, 1, (0, 2), (0, 2))
-        cast_w(nc.scalar.copy, 1, (0, 2), (2, 4))
-        cast_w(nc.vector.tensor_copy, 1, (2, 4), (0, 1), (0, P // 2))
-        cast_w(nc.scalar.copy, 1, (2, 4), (0, 1), (P // 2, P))
-        cast_w(nc.vector.tensor_copy, 1, (2, 4), (1, 2))
-        cast_w(nc.scalar.copy, 1, (2, 4), (2, 4))
-        quantize_w(1, 0, 1, "wc10")
-        quantize_w(1, 1, 2, "wc11")
-        product(1, 0, acc0[0], 0, S // 2)
-        product(1, 0, acc0[1], S // 2, S)
-        nc.vector.tensor_copy(h[0][:, 0 : S // 2], acc0[0][:])
-        nc.scalar.copy(h[0][:, S // 2 : S], acc0[1][:])
-        quantize_w(1, 2, 4, "wc10")
-        for t in range(1, TILES):
-            product(1, t, acc[t], 0, S)
-        nc.scalar.copy(h[1][:], acc[1][:])
-        for lo, hi in ((0, 384), (384, S)):
-            for t in (2, 3):
-                nc.scalar.copy(h[t][:, lo:hi], acc[t][:, lo:hi])
+        for half in range(2):
+            round_w(nc.vector.tensor_copy, 1, half, 0)
+            round_w(nc.scalar.copy, 1, half, 1)
+        quantize_w(1, 0, 1)
+        quantize_w(1, 1, 2)
+        quantize_w(1, 2, 4)
+        for t in range(TILES):
+            product(1, t)
+        for t in range(2):
+            nc.vector.tensor_copy(h[t][:, 0 : S // 2], acc[t, 0][:])
+            nc.scalar.copy(h[t][:, S // 2 : S], acc[t, S // 2][:])
+        for t in range(2, TILES):
+            nc.scalar.copy(h[t][:], acc[t, 0][:])
 
-        window = keep.tile([P, S], F32, name="window")
-        cols = HALF // 16
+        def entries(list_sb, lo, hi):
+            return list_sb[:, lo // 16 : hi // 16]
 
-        def entries(list_sb, c):
-            return list_sb[:, c * cols : (c + 1) * cols]
+        gated = keep.tile([P, TILES, V], F32, name="gated", align_bytes=64)
+        plain = [
+            keep.tile([P, TILES, HALF], F32, name="plain0", align_bytes=64),
+            keep.tile([P, TILES, HALF], F32, name="plain1", tag="wc12", align_bytes=64),
+        ]
 
-        gated_at = [[0, 1, 2, 3], [8, 9, 8, 7]]
-        z_at = [4, 2]
+        def second_member(t, lo, hi):
+            nc.vector.tensor_tensor(gated[:, t, lo:hi], h[t][:].indirect(entries(kb_sb, lo, hi)), gate_sb[:, lo:hi], MULT)
 
-        def second_member(c, t):
-            nc.vector.tensor_tensor(work[:, gated_at[c][t], :], h[t][:].indirect(entries(kb_sb, c)), gates[c], MULT)
+        def first_member(c, t):
+            nc.scalar.activation(plain[c][:, t, :], h[t][:].indirect(entries(ka_sb, c * HALF, (c + 1) * HALF)), COPY)
 
-        def first_member(c, t, lo=0, hi=HALF):
-            offsets = ka_sb[:, (c * HALF + lo) // 16 : (c * HALF + hi) // 16]
-            nc.vector.tensor_tensor(work[:, z_at[c] + t, lo:hi], h[t][:].indirect(offsets), work[:, gated_at[c][t], lo:hi], ADD)
+        for t in range(TILES):
+            second_member(t, 0, V)
+        for c in range(2):
+            for t in range(TILES):
+                first_member(c, t)
 
-        def interleave(c, z_bf, lo, hi, first=0, last=HALF):
-            nc.scalar.copy(
-                z_bf[:, PACK * first : PACK * last].rearrange("p (v i t) -> p v t i", i=4, t=PACK)[:, :, lo:hi, :],
-                work[:, z_at[c] + lo : z_at[c] + hi, first:last].rearrange("p t (v i) -> p v t i", i=4),
+        def merge_pairs(lo, hi):
+            z_bf = keep.tile([P, (hi - lo) * PACK], BF16, name="z_bf%d" % lo, tag="z_bf", align_bytes=64)
+            nc.vector.tensor_tensor(
+                z_bf[:].rearrange("p (v i t) -> p v t i", i=4, t=PACK),
+                plain[lo // HALF][:, :, lo % HALF : lo % HALF + hi - lo].rearrange("p t (v i) -> p v t i", i=4),
+                gated[:, :, lo:hi].rearrange("p t (v i) -> p v t i", i=4),
+                ADD,
             )
+            return z_bf
 
-        def second_product(c, z_bf):
-            zc = keep.tile([P, HALF], U32, name="zc%d" % c, align_bytes=64)
-            zs = keep.tile([P, HALF], U8, name="zs%d" % c, align_bytes=64)
+        def second_product(z_bf, lo, hi, bank):
+            zc = keep.tile([P, hi - lo], U32, name="zc%d" % lo, align_bytes=64)
+            zs = keep.tile([P, hi - lo], U8, name="zs%d" % lo, align_bytes=64)
             nc.vector.quantize_mx(out=zc[:].bitcast(FP8X4), scales=zs[:], in_=z_bf[:])
-            y_acc = psum.tile([P, HALF], F32, name="y_acc%d" % c, tag="bank%d" % (TILES + c))
+            y_acc = psum.tile([P, hi - lo], F32, name="y_acc%d" % lo, tag=bank)
             nc.tensor.matmul_mx(
                 out=y_acc[:],
                 lhsT=w2c[:].bitcast(FP8X4),
@@ -202,38 +205,20 @@ def tile_picked_zunm_none_p_kernel(
             )
             return y_acc
 
-        for t in range(2):
-            second_member(0, t)
-            second_member(1, t)
-            first_member(0, t)
-        second_member(0, 2)
-        second_member(0, 3)
-        first_member(0, 2)
-        first_member(0, 3)
-        z_bf = keep.tile([P, HALF * PACK], BF16, name="z_bf0", align_bytes=64)
-        interleave(0, z_bf, 0, 2)
-        interleave(0, z_bf, 2, 4)
-        first_member(1, 0)
-        first_member(1, 1)
-        second_member(1, 2)
-        y_acc0 = second_product(0, z_bf)
-        y0 = keep.tile([P, HALF], F32, name="y0")
-        nc.scalar.copy(y0[:], y_acc0[:])
-        second_member(1, 3)
-        z_bf = keep.tile([P, HALF * PACK], BF16, name="z_bf1", tag="zc0", align_bytes=64)
-        for first in (0, HALF // 2):
-            first_member(1, 2, first, first + HALF // 2)
-            first_member(1, 3, first, first + HALF // 2)
-            interleave(1, z_bf, 0, 4, first, first + HALF // 2)
-        nc.vector.tensor_copy(window[:].indirect(entries(ka_sb, 0)), y0[:])
-        y_acc1 = second_product(1, z_bf)
-        y0_again = work[:, z_at[1], :]
-        nc.scalar.copy(y0_again, y_acc0[:])
-        y1 = keep.tile([P, HALF], F32, name="y1")
-        nc.scalar.copy(y1[:], y_acc1[:])
-        nc.vector.tensor_tensor(window[:].indirect(entries(kb_sb, 0)), y0_again, back_sb[:, 0:HALF], MULT)
-        y1b = keep.tile([P, HALF], F32, name="y1b")
-        nc.vector.tensor_tensor(y1b[:], y_acc1[:], back_sb[:, HALF:V], MULT)
-        nc.vector.tensor_copy(window[:].indirect(entries(ka_sb, 1)), y1[:])
-        nc.vector.tensor_copy(window[:].indirect(entries(kb_sb, 1)), y1b[:])
-        nc.sync.dma_start(out, window[:])
+        y = keep.tile([P, V], F32, name="y", align_bytes=64)
+
+        def put_back(lo, hi):
+            nc.scalar.activation(first_win[:].indirect(entries(ka_sb, lo, hi)), y[:, lo:hi], COPY)
+            nc.vector.tensor_tensor(second_win[:].indirect(entries(kb_sb, lo, hi)), y[:, lo:hi], back_sb[:, lo:hi], MULT)
+
+        z0 = merge_pairs(0, HALF)
+        y_acc0 = second_product(z0, 0, HALF, "bank_y0")
+        z1 = merge_pairs(HALF, V)
+        y_acc1 = second_product(z1, HALF, V, "bank_y1")
+        nc.scalar.copy(y[:, 0:HALF], y_acc0[:])
+        put_back(0, HALF)
+        nc.scalar.copy(y[:, HALF:V], y_acc1[:])
+        put_back(HALF, V)
+        result = keep.tile([P, S], F32, name="result", align_bytes=64)
+        nc.vector.tensor_tensor(result[:], first_win[:], second_win[:], ADD)
+        nc.sync.dma_start(out, result[:])

@@ -95,10 +95,13 @@ def tile_picked_zunm_none_p_kernel(
         def gather_words(g):
             nc.vector.tensor_copy(xw[g][:], xw_all[g][:].bitcast(U32).indirect(offs_sb[:]))
 
-        def round_w(engine_copy, g, half, pair):
+        def round_w(engine_copy, g, half, t_lo, t_hi):
+            pair = t_lo // 2
             engine_copy(
-                w_bf[g, pair][:].rearrange("p (t m j) -> p m j t", t=2, j=PACK)[:, :, 2 * half : 2 * half + 2, :],
-                w_raw[g, half][:].rearrange("p j (m t) -> p m j t", t=PACK)[:, :, :, 2 * pair : 2 * pair + 2],
+                w_bf[g, pair][:].rearrange("p (t m j) -> p m j t", t=2, j=PACK)[
+                    :, :, 2 * half : 2 * half + 2, t_lo - 2 * pair : t_hi - 2 * pair
+                ],
+                w_raw[g, half][:].rearrange("p j (m t) -> p m j t", t=PACK)[:, :, :, t_lo:t_hi],
             )
 
         def quantize_w(g, t_lo, t_hi):
@@ -135,18 +138,19 @@ def tile_picked_zunm_none_p_kernel(
 
         gather_words(0)
         nc.vector.tensor_copy(xs[:], xs_all[:].indirect(offs_sb[:]))
-        round_w(nc.vector.tensor_copy, 0, 0, 0)
-        round_w(nc.scalar.copy, 0, 0, 1)
-        round_w(nc.vector.tensor_copy, 0, 1, 0)
-        round_w(nc.scalar.copy, 0, 1, 1)
+        for half in range(2):
+            round_w(nc.vector.tensor_copy, 0, half, 0, 2)
+            round_w(nc.scalar.copy, 0, half, 2, 4)
         quantize_w(0, 0, 2)
         quantize_w(0, 2, 4)
         for t in range(TILES):
             product(0, t)
         gather_words(1)
-        for half in range(2):
-            round_w(nc.vector.tensor_copy, 1, half, 0)
-            round_w(nc.scalar.copy, 1, half, 1)
+        round_w(nc.vector.tensor_copy, 1, 0, 0, 2)
+        round_w(nc.scalar.copy, 1, 0, 2, 4)
+        round_w(nc.vector.tensor_copy, 1, 1, 0, 1)
+        round_w(nc.vector.tensor_copy, 1, 1, 1, 2)
+        round_w(nc.scalar.copy, 1, 1, 2, 4)
         quantize_w(1, 0, 1)
         quantize_w(1, 1, 2)
         quantize_w(1, 2, 4)
@@ -179,21 +183,27 @@ def tile_picked_zunm_none_p_kernel(
             for t in range(TILES):
                 first_member(c, t)
 
-        def merge_pairs(lo, hi):
-            z_bf = keep.tile([P, (hi - lo) * PACK], BF16, name="z_bf%d" % lo, tag="z_bf", align_bytes=64)
-            nc.vector.tensor_tensor(
-                z_bf[:].rearrange("p (v i t) -> p v t i", i=4, t=PACK),
-                plain[lo // HALF][:, :, lo % HALF : lo % HALF + hi - lo].rearrange("p t (v i) -> p v t i", i=4),
-                gated[:, :, lo:hi].rearrange("p t (v i) -> p v t i", i=4),
-                ADD,
-            )
-            return z_bf
+        QUARTER = HALF // 2
 
-        def second_product(z_bf, lo, hi, bank):
-            zc = keep.tile([P, hi - lo], U32, name="zc%d" % lo, align_bytes=64)
-            zs = keep.tile([P, hi - lo], U8, name="zs%d" % lo, align_bytes=64)
-            nc.vector.quantize_mx(out=zc[:].bitcast(FP8X4), scales=zs[:], in_=z_bf[:])
-            y_acc = psum.tile([P, hi - lo], F32, name="y_acc%d" % lo, tag=bank)
+        def second_product(c):
+            z_tile = keep.tile([P, HALF * PACK], BF16, name="z_bf%d" % c, tag="z_bf", align_bytes=64)
+            z_bf = [z_tile[:, PACK * lo : PACK * (lo + QUARTER)] for lo in (0, QUARTER)]
+            zc = keep.tile([P, HALF], U32, name="zc%d" % c, align_bytes=64)
+            zs = keep.tile([P, HALF], U8, name="zs%d" % c, align_bytes=64)
+            for piece in range(2):
+                lo = piece * QUARTER
+                nc.vector.tensor_tensor(
+                    z_bf[piece].rearrange("p (v i t) -> p v t i", i=4, t=PACK),
+                    plain[c][:, :, lo : lo + QUARTER].rearrange("p t (v i) -> p v t i", i=4),
+                    gated[:, :, c * HALF + lo : c * HALF + lo + QUARTER].rearrange("p t (v i) -> p v t i", i=4),
+                    ADD,
+                )
+            for piece in range(2):
+                lo = piece * QUARTER
+                nc.vector.quantize_mx(
+                    out=zc[:, lo : lo + QUARTER].bitcast(FP8X4), scales=zs[:, lo : lo + QUARTER], in_=z_bf[piece]
+                )
+            y_acc = psum.tile([P, HALF], F32, name="y_acc%d" % c, tag="bank_y%d" % c)
             nc.tensor.matmul_mx(
                 out=y_acc[:],
                 lhsT=w2c[:].bitcast(FP8X4),
@@ -207,18 +217,20 @@ def tile_picked_zunm_none_p_kernel(
 
         y = keep.tile([P, V], F32, name="y", align_bytes=64)
 
-        def put_back(lo, hi):
-            nc.scalar.activation(first_win[:].indirect(entries(ka_sb, lo, hi)), y[:, lo:hi], COPY)
-            nc.vector.tensor_tensor(second_win[:].indirect(entries(kb_sb, lo, hi)), y[:, lo:hi], back_sb[:, lo:hi], MULT)
+        windows = [first_win, second_win]
 
-        z0 = merge_pairs(0, HALF)
-        y_acc0 = second_product(z0, 0, HALF, "bank_y0")
-        z1 = merge_pairs(HALF, V)
-        y_acc1 = second_product(z1, HALF, V, "bank_y1")
+        def put_back(c):
+            lo, hi = c * HALF, (c + 1) * HALF
+            nc.scalar.activation(windows[c][:].indirect(entries(ka_sb, lo, hi)), y[:, lo:hi], COPY)
+            nc.vector.tensor_tensor(windows[1 - c][:].indirect(entries(kb_sb, lo, hi)), y[:, lo:hi], back_sb[:, lo:hi], MULT)
+
+        y_acc0 = second_product(0)
+        y_acc1 = second_product(1)
         nc.scalar.copy(y[:, 0:HALF], y_acc0[:])
-        put_back(0, HALF)
+        put_back(0)
         nc.scalar.copy(y[:, HALF:V], y_acc1[:])
-        put_back(HALF, V)
-        result = keep.tile([P, S], F32, name="result", align_bytes=64)
-        nc.vector.tensor_tensor(result[:], first_win[:], second_win[:], ADD)
-        nc.sync.dma_start(out, result[:])
+        put_back(1)
+        for lo in (0, S // 2):
+            result = keep.tile([P, S // 2], F32, name="result%d" % lo, align_bytes=64)
+            nc.vector.tensor_tensor(result[:], first_win[:, lo : lo + S // 2], second_win[:, lo : lo + S // 2], ADD)
+            nc.sync.dma_start(out[:, lo : lo + S // 2], result[:])

@@ -193,9 +193,9 @@ def tile_picked_zunm_none_p_kernel(
             for piece in range(2):
                 lo = piece * QUARTER
                 nc.vector.tensor_tensor(
-                    z_bf[piece].rearrange("p (v i t) -> p v t i", i=4, t=PACK),
-                    plain[c][:, :, lo : lo + QUARTER].rearrange("p t (v i) -> p v t i", i=4),
-                    gated[:, :, c * HALF + lo : c * HALF + lo + QUARTER].rearrange("p t (v i) -> p v t i", i=4),
+                    z_bf[piece].rearrange("p (v i t) -> p v t i", i=2, t=PACK),
+                    plain[c][:, :, lo : lo + QUARTER].rearrange("p t (v i) -> p v t i", i=2),
+                    gated[:, :, c * HALF + lo : c * HALF + lo + QUARTER].rearrange("p t (v i) -> p v t i", i=2),
                     ADD,
                 )
             for piece in range(2):

@@ -230,7 +230,7 @@ def tile_picked_zunm_none_p_kernel(
         put_back(0)
         nc.scalar.copy(y[:, HALF:V], y_acc1[:])
         put_back(1)
-        for lo in (0, S // 2):
-            result = keep.tile([P, S // 2], F32, name="result%d" % lo, align_bytes=64)
-            nc.vector.tensor_tensor(result[:], first_win[:, lo : lo + S // 2], second_win[:, lo : lo + S // 2], ADD)
-            nc.sync.dma_start(out[:, lo : lo + S // 2], result[:])
+        for lo, hi in [(lo, lo + P) for lo in range(0, S, P)]:
+            result = keep.tile([P, hi - lo], F32, name="result%d" % lo, align_bytes=64)
+            nc.vector.tensor_tensor(result[:], first_win[:, lo:hi], second_win[:, lo:hi], ADD)
+            (nc.sync if lo % (2 * P) == 0 else nc.scalar).dma_start(out[:, lo:hi], result[:])

@@ -34,17 +34,17 @@ def tile_picked_zunm_none_p_kernel(
         offs_sb = keep.tile([P, S // 16], U16, name="offs_sb")
         ka_sb = keep.tile([P, V // 16], U16, name="ka_sb")
         kb_sb = keep.tile([P, V // 16], U16, name="kb_sb")
-        xs_all = keep.tile([P, T], U8, name="xs_all", align_bytes=64)
-        w2s = keep.tile([P, N], U8, name="w2s", align_bytes=64)
-        w2c = keep.tile([P, N], I32, name="w2c", align_bytes=64)
-        xw_all = [keep.tile([P, T], I32, name="xw_all%d" % g, align_bytes=64) for g in range(PASSES)]
+        xs_all = keep.tile([P, T], U8, name="xs_all", align_bytes=256)
+        w2s = keep.tile([P, N], U8, name="w2s", align_bytes=256)
+        w2c = keep.tile([P, N], I32, name="w2c", align_bytes=256)
+        xw_all = [keep.tile([P, T], I32, name="xw_all%d" % g, align_bytes=256) for g in range(PASSES)]
         w_raw = {
-            (g, half): keep.tile([P, 2, H], F32, name="w_raw%d%d" % (g, half), align_bytes=64)
+            (g, half): keep.tile([P, 2, H], F32, name="w_raw%d%d" % (g, half), align_bytes=256)
             for g in range(PASSES)
             for half in range(2)
         }
-        gate_sb = keep.tile([P, V], F32, name="gate_sb", align_bytes=64)
-        back_sb = keep.tile([P, V], F32, name="back_sb", align_bytes=64)
+        gate_sb = keep.tile([P, V], F32, name="gate_sb", align_bytes=256)
+        back_sb = keep.tile([P, V], F32, name="back_sb", align_bytes=256)
         first_win = keep.tile([P, S], F32, name="first_win", align_bytes=64)
         second_win = keep.tile([P, S], F32, name="second_win", align_bytes=64)
 
@@ -231,6 +231,6 @@ def tile_picked_zunm_none_p_kernel(
         nc.scalar.copy(y[:, HALF:V], y_acc1[:])
         put_back(1)
         for lo, hi in [(lo, lo + P) for lo in range(0, S, P)]:
-            result = keep.tile([P, hi - lo], F32, name="result%d" % lo, align_bytes=64)
+            result = keep.tile([P, hi - lo], F32, name="result%d" % lo, align_bytes=256)
             nc.vector.tensor_tensor(result[:], first_win[:, lo:hi], second_win[:, lo:hi], ADD)
             (nc.sync if lo % (2 * P) == 0 else nc.scalar).dma_start(out[:, lo:hi], result[:])

from contextlib import ExitStack

import concourse.mybir as mybir

K, T, S, H, N, V = 1024, 1024, 512, 512, 128, 256
FLOPS = 2 * K * H * S + 2 * H * N * V

F32 = mybir.dt.float32
BF16 = mybir.dt.bfloat16
I32 = mybir.dt.int32
U32 = mybir.dt.uint32
U16 = mybir.dt.uint16
U8 = mybir.dt.uint8
FP8X4 = mybir.dt.float8_e4m3fn_x4
MULT = mybir.AluOpType.mult
ADD = mybir.AluOpType.add
COPY = mybir.ActivationFunctionType.Copy

P = 128
PACK = 4
PASSES = K // (P * PACK)
HALF = V // 2
TILES = H // P


def tile_picked_zunm_none_p_kernel(
    tc, x_words, x_scales, w1, w2_words, w2_scales, gate, back, offs, ka, kb, out
):
    nc = tc.nc
    with ExitStack() as ctx:
        keep = ctx.enter_context(tc.tile_pool(name="keep", bufs=1))
        psum = ctx.enter_context(tc.psum_pool(name="psum", bufs=1))

        offs_sb = keep.tile([P, S // 16], U16, name="offs_sb")
        ka_sb = keep.tile([P, V // 16], U16, name="ka_sb")
        kb_sb = keep.tile([P, V // 16], U16, name="kb_sb")
        xs_all = keep.tile([P, T], U8, name="xs_all", align_bytes=256)
        w2s = keep.tile([P, N], U8, name="w2s", align_bytes=256)
        w2c = keep.tile([P, N], I32, name="w2c", align_bytes=256)
        xw_all = [keep.tile([P, T], I32, name="xw_all%d" % g, align_bytes=256) for g in range(PASSES)]
        w_raw = {
            (g, half): keep.tile([P, 2, H], F32, name="w_raw%d%d" % (g, half), align_bytes=256)
            for g in range(PASSES)
            for half in range(2)
        }
        gate_sb = keep.tile([P, V], F32, name="gate_sb", align_bytes=256)
        back_sb = keep.tile([P, V], F32, name="back_sb", align_bytes=256)
        first_win = keep.tile([P, S], F32, name="first_win", align_bytes=64)
        second_win = keep.tile([P, S], F32, name="second_win", align_bytes=64)

        nc.vector.memset(xs_all[:].bitcast(I32), 0)
        nc.vector.memset(w2s[:].bitcast(I32), 0)
        nc.vector.memset(first_win[:], 0.0)
        nc.vector.memset(second_win[:], 0.0)

        def load_words(g):
            nc.sync.dma_start(xw_all[g][:], x_words[g].rearrange("p n t -> p (n t)").bitcast(I32))

        def load_w(g, half):
            rows = w1[512 * g : 512 * (g + 1), :].rearrange("(p j) c -> p j c", j=PACK)
            nc.sync.dma_start(w_raw[g, half][:], rows[:, 2 * half : 2 * half + 2, :])

        load_words(0)
        nc.sync.dma_start(offs_sb[:], offs)
        load_w(0, 0)
        for q in range(4):
            nc.sync.dma_start(
                xs_all[32 * q : 32 * q + 8, :].bitcast(I32),
                x_scales[:, 4 * q : 4 * q + 4, :].bitcast(I32),
            )
        load_w(0, 1)
        load_words(1)
        load_w(1, 0)
        load_w(1, 1)
        nc.sync.dma_start(kb_sb[:], kb)
        nc.sync.dma_start(gate_sb[:], gate)
        nc.sync.dma_start(ka_sb[:], ka)
        nc.sync.dma_start(w2c[:], w2_words[0].rearrange("p n t -> p (n t)").bitcast(I32))
        for q in range(4):
            nc.sync.dma_start(
                w2s[32 * q : 32 * q + 4, :].bitcast(I32),
                w2_scales[0, 4 * q : 4 * q + 4, :].bitcast(I32),
            )
        nc.sync.dma_start(back_sb[:], back)

        xw = [keep.tile([P, S], U32, name="xw%d" % g, align_bytes=64) for g in range(PASSES)]
        xs = keep.tile([P, S], U8, name="xs", align_bytes=64)
        w_bf = {
            (g, pair): keep.tile([P, 2 * H], BF16, name="w_bf%d%d" % (g, pair), align_bytes=64)
            for g in range(PASSES)
            for pair in range(2)
        }
        wc, ws = {}, {}

        def gather_words(g):
            nc.vector.tensor_copy(xw[g][:], xw_all[g][:].bitcast(U32).indirect(offs_sb[:]))

        def round_w(engine_copy, g, half, t_lo, t_hi):
            pair = t_lo // 2
            engine_copy(
                w_bf[g, pair][:].rearrange("p (t m j) -> p m j t", t=2, j=PACK)[
                    :, :, 2 * half : 2 * half + 2, t_lo - 2 * pair : t_hi - 2 * pair
                ],
                w_raw[g, half][:].rearrange("p j (m t) -> p m j t", t=PACK)[:, :, :, t_lo:t_hi],
            )

        def quantize_w(g, t_lo, t_hi):
            width = P * (t_hi - t_lo)
            codes = keep.tile([P, width], U32, name="wc%d%d" % (g, t_lo), tag="wc%d%d" % (g, t_lo), align_bytes=64)
            scales = keep.tile([P, width], U8, name="ws%d%d" % (g, t_lo), align_bytes=64)
            first = H * (t_lo % 2)
            nc.vector.quantize_mx(
                out=codes[:].bitcast(FP8X4), scales=scales[:], in_=w_bf[g, t_lo // 2][:, first : first + PACK * width]
            )
            for t in range(t_lo, t_hi):
                wc[g, t] = codes[:, P * (t - t_lo) : P * (t - t_lo + 1)]
                ws[g, t] = scales[:, P * (t - t_lo) : P * (t - t_lo + 1)]

        cuts = [[(0, S // 2), (S // 2, S)], [(0, S // 2), (S // 2, S)], [(0, S)], [(0, S)]]
        acc = {
            (t, lo): psum.tile([P, hi - lo], F32, name="acc%d_%d" % (t, lo), tag="bank%d_%d" % (t, lo))
            for t in range(TILES)
            for lo, hi in cuts[t]
        }
        h = [keep.tile([P, S], F32, name="h%d" % t, align_bytes=64) for t in range(TILES)]

        def product(g, t):
            for lo, hi in cuts[t]:
                nc.tensor.matmul_mx(
                    out=acc[t, lo][:],
                    lhsT=wc[g, t].bitcast(FP8X4),
                    lhsT_scale=ws[g, t],
                    rhs=xw[g][:, lo:hi].bitcast(FP8X4),
                    rhs_scale=xs[4 * g : P, lo:hi],
                    start=(g == 0),
                    stop=(g == PASSES - 1),
                )

        gather_words(0)
        nc.vector.tensor_copy(xs[:], xs_all[:].indirect(offs_sb[:]))
        for half in range(2):
            round_w(nc.vector.tensor_copy, 0, half, 0, 2)
            round_w(nc.scalar.copy, 0, half, 2, 4)
        quantize_w(0, 0, 2)
        quantize_w(0, 2, 4)
        for t in range(TILES):
            product(0, t)
        gather_words(1)
        round_w(nc.vector.tensor_copy, 1, 0, 0, 2)
        round_w(nc.scalar.copy, 1, 0, 2, 4)
        round_w(nc.vector.tensor_copy, 1, 1, 0, 1)
        round_w(nc.vector.tensor_copy, 1, 1, 1, 2)
        round_w(nc.scalar.copy, 1, 1, 2, 4)
        quantize_w(1, 0, 1)
        quantize_w(1, 1, 2)
        quantize_w(1, 2, 4)
        for t in range(TILES):
            product(1, t)
        for t in range(2):
            nc.vector.tensor_copy(h[t][:, 0 : S // 2], acc[t, 0][:])
            nc.scalar.copy(h[t][:, S // 2 : S], acc[t, S // 2][:])
        for t in range(2, TILES):
            nc.scalar.copy(h[t][:], acc[t, 0][:])

        def entries(list_sb, lo, hi):
            return list_sb[:, lo // 16 : hi // 16]

        gated = keep.tile([P, TILES, V], F32, name="gated", align_bytes=64)
        plain = [
            keep.tile([P, TILES, HALF], F32, name="plain0", align_bytes=64),
            keep.tile([P, TILES, HALF], F32, name="plain1", tag="wc12", align_bytes=64),
        ]

        def second_member(t, lo, hi):
            nc.vector.tensor_tensor(gated[:, t, lo:hi], h[t][:].indirect(entries(kb_sb, lo, hi)), gate_sb[:, lo:hi], MULT)

        def first_member(c, t):
            nc.scalar.activation(plain[c][:, t, :], h[t][:].indirect(entries(ka_sb, c * HALF, (c + 1) * HALF)), COPY)

        for t in range(TILES):
            second_member(t, 0, V)
        for c in range(2):
            for t in range(TILES):
                first_member(c, t)

        QUARTER = HALF // 2

        def second_product(c):
            z_tile = keep.tile([P, HALF * PACK], BF16, name="z_bf%d" % c, tag="z_bf", align_bytes=64)
            z_bf = [z_tile[:, PACK * lo : PACK * (lo + QUARTER)] for lo in (0, QUARTER)]
            zc = keep.tile([P, HALF], U32, name="zc%d" % c, align_bytes=64)
            zs = keep.tile([P, HALF], U8, name="zs%d" % c, align_bytes=64)
            for piece in range(2):
                lo = piece * QUARTER
                nc.vector.tensor_tensor(
                    z_bf[piece].rearrange("p (v i t) -> p v t i", i=2, t=PACK),
                    plain[c][:, :, lo : lo + QUARTER].rearrange("p t (v i) -> p v t i", i=2),
                    gated[:, :, c * HALF + lo : c * HALF + lo + QUARTER].rearrange("p t (v i) -> p v t i", i=2),
                    ADD,
                )
            for piece in range(2):
                lo = piece * QUARTER
                nc.vector.quantize_mx(
                    out=zc[:, lo : lo + QUARTER].bitcast(FP8X4), scales=zs[:, lo : lo + QUARTER], in_=z_bf[piece]
                )
            y_acc = psum.tile([P, HALF], F32, name="y_acc%d" % c, tag="bank_y%d" % c)
            nc.tensor.matmul_mx(
                out=y_acc[:],
                lhsT=w2c[:].bitcast(FP8X4),
                lhsT_scale=w2s[:],
                rhs=zc[:].bitcast(FP8X4),
                rhs_scale=zs[:],
                start=True,
                stop=True,
            )
            return y_acc

        y = keep.tile([P, V], F32, name="y", align_bytes=64)

        windows = [first_win, second_win]

        def put_back(c):
            lo, hi = c * HALF, (c + 1) * HALF
            nc.scalar.activation(windows[c][:].indirect(entries(ka_sb, lo, hi)), y[:, lo:hi], COPY)
            nc.vector.tensor_tensor(windows[1 - c][:].indirect(entries(kb_sb, lo, hi)), y[:, lo:hi], back_sb[:, lo:hi], MULT)

        y_acc0 = second_product(0)
        y_acc1 = second_product(1)
        nc.scalar.copy(y[:, 0:HALF], y_acc0[:])
        put_back(0)
        nc.scalar.copy(y[:, HALF:V], y_acc1[:])
        put_back(1)
        for lo, hi in [(lo, lo + P) for lo in range(0, S, P)]:
            result = keep.tile([P, hi - lo], F32, name="result%d" % lo, align_bytes=256)
            nc.vector.tensor_tensor(result[:], first_win[:, lo:hi], second_win[:, lo:hi], ADD)
            (nc.sync if lo % (2 * P) == 0 else nc.scalar).dma_start(out[:, lo:hi], result[:])
